import numpy as np, ml_dtypes
CORES = [3,11,19,27,35,43,51,59]
N = 8
BF = ml_dtypes.bfloat16
W, P, L, SH, RO = 2048, 256, 32, 4, 3
def parts(rng):
    return (rng.integers(0, 256, (N, 8, 16, W)), rng.integers(0, W, (N, 8, 16, P)), rng.integers(0, W, (N, 8, 16, P)),
            rng.integers(500, 1300, (N, 8, 16)), rng.integers(30, 100, (N, 8, 16)))
def pack(x, r, m, t, e):
    return {"flood": np.ascontiguousarray(x.reshape(N, 128, W)).astype(np.float32).astype(BF), "riv": np.ascontiguousarray(r.reshape(N, 128, P)).astype(np.int32),
            "bord": np.ascontiguousarray(m.reshape(N, 128, P)).astype(np.int32), "th": t.reshape(N, 128, 1).astype(np.int32), "eps": e.reshape(N, 128, 1).astype(np.int32)}
def setup_inputs(rng):
    return pack(*parts(rng))
def setup_inputs_spread(rng):
    x = np.minimum((np.exp2(3 + 5.5 * rng.random((N, 8, 1, W))) * rng.random((N, 8, 16, W))).astype(np.int64), 255)
    r = (W * rng.random((N, 8, 16, P)) ** 3).astype(np.int64); m = W - 1 - (W * rng.random((N, 8, 16, P)) ** 3).astype(np.int64)
    t = np.minimum(np.exp2(7 + 5 * rng.random((N, 8, 16))).astype(np.int64), 4080); e = np.minimum(np.exp2(8 * rng.random((N, 8, 16))).astype(np.int64) - 1, 255)
    return pack(x, r, m, t, e)
def setup_inputs_ends(rng):
    x = 255 * rng.integers(0, 2, (N, 8, 16, W)); pure = 255 * rng.integers(0, 2, (N, 8, 1, W))
    kind = rng.random((N, 8)) < 0.4; kind[:, 7] = True
    x = np.where(kind[:, :, None, None], pure, x)
    k2 = (((W - 1) * (W - 1) >> SH) + 38 * (W - 1)) & (W - 1)
    x[:, 7, :, 0] = 0
    for c in (W - 1, W - 37, k2): x[:, 7, :, c] = 255
    r = (W - 1) * rng.integers(0, 2, (N, 8, 16, P)); m = (W - 1) * rng.integers(0, 2, (N, 8, 16, P))
    t = 4080 * rng.integers(0, 2, (N, 8, 16)); t[:, :, 2] = 0; t[:, :, 5] = 4080
    e = np.zeros((N, 8, 16), np.int64)
    for q in range(N):
        for g in range(8):
            n = int(rng.choice(np.array([0, 7, 8, 8, 9, 9, 16])))
            if g == 7: n = 8 + q % 2
            e[q, g, rng.permutation(16)[:n]] = 255
    for p in (1, 8, 15):
        r[:, 7, p] = np.where((np.arange(P) // L) % 2 == 0, W - 1, 0); m[:, 7, p] = W - 1; t[:, 7, p] = 4080
    for p in (0, 3, 14):
        r[:, 7, p] = W - 1; r[:, 7, p, P - 1] = 0; m[:, 7, p] = W - 1
    t[:, 7, 0] = 0; t[:, 7, 14] = 0
    r[:, 7, 10] = ((W - 1) * (np.arange(N) % 2))[:, None]; m[:, 7, 10] = W - 1; t[:, 7, 10] = 4080
    return pack(x, r, m, t, e)
def setup_inputs_corners(rng):
    x, r, m, t, e = parts(rng)
    r = np.argsort(rng.random((N, 8, 16, W)), axis=-1)[..., :P]; r = np.ascontiguousarray(r)
    kd = rng.integers(0, 7, (N, 8, 16)); kd[:, 0] = 6; kd[0::2, 3] = 0; kd[1::2, 3] = 6; kd[:, 7, 14] = 5; kd[:, 7, 15] = 2
    r[..., L] = np.where((kd == 1) | (kd == 3), r[..., 0], r[..., L])
    r[..., P - 1] = np.where((kd == 2) | (kd == 3), r[..., P - 1 - L], r[..., P - 1])
    m = np.where(rng.random((N, 8, 16, P)) < 0.3, r, m); e = np.zeros((N, 8, 16), np.int64)
    for q in range(N):
        for g in range(8):
            k = 8 if g in (0, 7) else int(rng.choice(np.array([7, 8, 8, 9]))); o = rng.permutation(16)
            x[q, g, o[:k]] = rng.integers(0, 256, (k, 1))
            n = max(0, 9 - k - int(rng.integers(0, 2))); e[q, g, o[k:k + n]] = 255
            v = x[q, g][:, r[q, g]]; s = np.min(np.add.reduce(np.abs(v[..., :P - L] - v[..., L:]), axis=0), axis=-1); c = kd[q, g]
            t[q, g] = np.where(c == 0, 0, np.where(c < 4, 1, np.where(c == 4, s, np.where(c == 5, np.minimum(s + 1, 4080), 4080))))
    return pack(x, r, m, t, e)
def setup_inputs_ties(rng):
    x = rng.integers(0, 4, (N, 8, 16, W)); r, m = rng.integers(0, W, (2, N, 8, 16, P))
    w = rng.integers(0, W, (N, 4, 1, 12)); w[..., 0] = 0; w[..., 11] = W - 1
    r[:, 1::2] = np.take_along_axis(np.broadcast_to(w, (N, 4, 16, 12)), rng.integers(0, 12, (N, 4, 16, P)), -1)
    m[:, ::2] = np.where(rng.random((N, 4, 16, P)) < 0.5, r[:, ::2], m[:, ::2])
    return pack(x, r, m, rng.integers(0, 18, (N, 8, 16)), rng.integers(0, 3, (N, 8, 16)))
def setup_inputs_far(rng):
    k = W // 16; n = W - 2 * k; pos = np.argsort(rng.random((N, 8, W)), axis=-1); o = np.argsort(pos, axis=-1)
    share = np.where(np.arange(8) % 2 == 0, 0.5, rng.choice(np.array([0.2, 0.8]), (N, 8)))
    hn = (share * n).astype(np.int64)[..., None]; high = (pos >= k) & (pos < 2 * k + hn)
    x = np.where((pos < 2 * k)[:, :, None], 0, rng.integers(0, 8, (N, 8, 16, W))); x = np.where(high[:, :, None], 255 - x, x)
    c = rng.integers(0, 2, (N, 8, 16, P)); c[:, :, ::2] = (np.arange(P) // L + rng.integers(0, 2, (N, 8, 8, 1))) % 2; c[:, :, 1::4, P - 1] = 0
    u = rng.random((N, 8, 16, P)); hn = hn[..., None]; odd = (np.arange(16) % 2 == 1)[:, None]
    mixed = np.where(c == 1, 2 * k + (u * hn).astype(np.int64), 2 * k + hn + (u * (n - hn)).astype(np.int64))
    i = np.where(odd, c * k + (u * k).astype(np.int64), mixed)
    r = np.take_along_axis(o, i.reshape(N, 8, -1), -1).reshape(N, 8, 16, P)
    i = (1 - c) * k + rng.integers(0, k, (N, 8, 16, P)); far = np.take_along_axis(o, i.reshape(N, 8, -1), -1).reshape(N, 8, 16, P)
    m = np.where(odd & (rng.random((N, 8, 16, P)) < 0.25), far, rng.integers(0, W, (N, 8, 16, P))); m[:, :, 1::4, P - 1] = far[:, :, 1::4, P - 1]
    t = rng.integers(3925, 3976, (N, 8, 16)); t[:, :, ::4] = 3929 + 4 * rng.integers(0, 12, (N, 8, 4)); t[:, :, 1::4] = 0; t[:, :, 3::4] = rng.integers(3900, 4080, (N, 8, 4))
    e = np.where(np.argsort(rng.random((N, 8, 16)), axis=-1) < 12, 254, rng.integers(247, 255, (N, 8, 16)))
    return pack(x, r, m, t, e)
def check_inputs(d):
    bad = []
    for k, lo, hi in (("flood", 0, 255), ("riv", 0, W - 1), ("bord", 0, W - 1), ("th", 0, 4080), ("eps", 0, 255)):
        v = np.asarray(d[k]).astype(np.float64)
        if not (np.all(v >= lo) and np.all(v <= hi)): bad.append("range of " + k)
        elif not np.all(v == np.floor(v)): bad.append("whole numbers in " + k)
    return bad
def columns(x, names):
    return np.take(x, names + W * np.arange(8)[:, None, None], axis=0)
def total(v):
    return np.add.reduce(v, axis=-1, dtype=np.int16)
def reference(flood, riv, bord, th, eps):
    R = riv.astype(np.int64).reshape(N, 8, 16, P); M = bord.astype(np.int64).reshape(N, 8, 16, P); A = np.zeros((N, 8, 16), np.int64)
    T = th.astype(np.int64).reshape(N, 8, 16); E = eps.astype(np.int16).reshape(N, 8, 1, 1, 16)
    X = [np.ascontiguousarray(a.astype(np.float32).astype(np.int16).reshape(8, 16, W).transpose(0, 2, 1)).reshape(8 * W, 16) for a in flood]
    place = np.arange(P)
    for t in range(RO):
        first = np.zeros((N, 8, 16), np.int64); loops = np.zeros((N, 8, 16, L), np.int64)
        for q in range(N):
            r, m = R[q], M[q]; h = r[..., :P - 1]; x = columns(X[q], r); nxt = x[:, :, 1:]; now = np.abs(x[:, :, :P - 1] - nxt)
            before = np.concatenate([r[..., :1], r[..., :P - 2]], axis=-1)
            cand = np.stack([((h * a >> SH) + 37 * h + a + 77 * t) & (W - 1) for a in (before, r[..., 1:], m[..., :P - 1], m[..., 1:])] + [m[..., :P - 1]])
            score = np.stack([total(np.abs(columns(X[q], c) - nxt)) for c in cand])
            best = np.take_along_axis(cand, np.argmin(score, axis=0)[None], 0)[0]
            near = total((np.abs(columns(X[q], best) - nxt) < now).astype(np.int16))
            R[q, :, :, :P - 1] = np.where(near >= 9, best, h)
            x = columns(X[q], R[q]); ok = total(np.abs(x[:, :, :P - L] - x[:, :, L:])) < (T[q] + 16 * A[q])[..., None]
            first[q] = np.where(np.any(ok, axis=-1), np.argmax(ok, axis=-1), P)
            loops[q] = np.take_along_axis(R[q], np.minimum(first[q] + 1, P - L)[..., None] + np.arange(L), -1)
        for q in range(N):
            src = (q - 1 - t % (N - 1)) % N
            lp = np.where((first[src] < P)[..., None], loops[src], loops[q])
            R[q] = np.take_along_axis(np.concatenate([R[q], lp], axis=-1), place + L * (place > first[q][..., None]), -1)
            A[q] = A[q] + (first[q] < P)
            near = total((np.abs(columns(X[q], R[q]) - columns(X[q], M[q])) <= E[q]).astype(np.int16))
            M[q] = np.where(near >= 9, R[q], M[q])
    return {"yr": R.reshape(N, 128, P).astype(np.float32), "ym": M.reshape(N, 128, P).astype(np.float32), "ya": A.reshape(N, 128, 1).astype(np.float32)}

@@ -1,0 +1,566 @@
+import numpy as np
+from concourse.mybir import dt, AluOpType, AxisListType, ActivationFunctionType
+
+OP = AluOpType
+N, W, P, L, ROUNDS = 8, 2048, 256, 32, 3
+CK = 64
+CE = 16 * CK
+BANK = 512
+
+_F, _B, _I, _U = "float32", "bfloat16", "int32", "uint16"
+SCRATCH = {
+    "fl": ("sbuf", [128, 2 * W], _B),
+    "xm": ("sbuf", [128, 4096], _B), "xp": ("sbuf", [128, 4096], _B),
+    "ones": ("sbuf", [128, 128], _B), "ident": ("sbuf", [128, 128], _B), "nident": ("sbuf", [128, 128], _B),
+    "g8": ("sbuf", [128, 8], _B), "g8b": ("sbuf", [128, 8], _B),
+    "b1": ("sbuf", [128, 144], _B), "b4096": ("sbuf", [128, 144], _B),
+    "b8192": ("sbuf", [128, 144], _B), "b16384": ("sbuf", [128, 144], _B),
+    "ck": ("sbuf", [128, 320], _B), "cy": ("sbuf", [128, 192], _B), "cz": ("sbuf", [128, 64], _B),
+    "iot": ("sbuf", [128, 256], _F), "i16": ("sbuf", [128, 64], _I), "ipt": ("sbuf", [128, 64], _I),
+    "ip2": ("sbuf", [128, 64], _I), "cpos": ("sbuf", [128, 64], _F),
+    "dgi": ("sbuf", [128, 512], _I), "dgj": ("sbuf", [128, 512], _I), "diag": ("sbuf", [128, 512], _F), "seg": ("sbuf", [128, 512], _F),
+    "thi": ("sbuf", [128, 1], _I), "epi": ("sbuf", [128, 1], _I), "epf": ("sbuf", [128, 1], _F),
+    "tha": ("sbuf", [128, 8], _F), "nk": ("sbuf", [128, 64], _F), "aout": ("sbuf", [128, 4], _F),
+    "ru0": ("sbuf", [128, 256], _U), "lu": ("sbuf", [128, 32], _U),
+    "lg": ("sbuf", [128, 512], _F), "ls": ("sbuf", [128, 512], _F),
+    "l1": ("sbuf", [128, 32], _F), "l2": ("sbuf", [128, 32], _F),
+    "yrf": ("sbuf", [128, 256], _F), "ymf": ("sbuf", [128, 256], _F),
+    "pv": ("psum", [128, 512], _F), "sc0": ("psum", [128, 512], _F), "sc1": ("psum", [128, 512], _F),
+    "cnt": ("psum", [128, 512], _F), "sub0": ("psum", [128, 1024], _F), "sub1": ("psum", [128, 1024], _F),
+}
+for _k in range(3):
+    SCRATCH["lout%d" % _k] = ("sbuf", [128, 32], _F)
+    SCRATCH["land%d" % _k] = ("sbuf", [128, 32], _F)
+for _k in range(2):
+    for _n, _c, _d in (("rn", 264, _I), ("rf", 264, _F), ("mn", 264, _I), ("mf", 264, _F), ("rp", 296, _I),
+                       ("rpu", 256, _U), ("r2u", 256, _U), ("mu", 256, _U), ("xr", 4112, _B),
+                       ("me", 64, _F), ("pr", 256, _I), ("v", 256, _I), ("u", 256, _U), ("xd", 4096, _B), ("win", 5120, _B),
+                       ("now", 1024, _B), ("nb", 1024, _B), ("kb", 128, _F), ("kc", 128, _F), ("k4", 64, _I), ("ka", 64, _I),
+                       ("kv", 64, _I), ("w", 64, _F), ("o", 64, _F), ("ou", 64, _U), ("d", 64, _F), ("rr", 64, _I),
+                       ("a2", 1024, _B), ("nf", 64, _F), ("q", 64, _F), ("df", 64, _F), ("a3", 1024, _B), ("c3", 1024, _B), ("mm", 64, _I)):
+        SCRATCH[_n + "_%d" % _k] = ("sbuf", [128, _c], _d)
+NDMA = 16
+SEMAPHORES = ["sV", "sS", "sP", "sG", "ls", "arr0", "arr1", "arr2"] + ["d%d" % k for k in range(NDMA)]
+
+CY = 0.00083 * 1.2
+GA = 1.5
+PEC = 0.0005
+WAKE = 0.06
+TAIL = 4 * ROUNDS - 2
+FIRST = ((0, 66, "S"), (66, 130, "V"), (130, 194, "S"), (194, 256, "S"))
+
+
+def _span(r):
+    return r[0], r[1], r[2]
+
+
+def _ap(T, r):
+    if len(r) == 4:
+        return T[r[0]][:, r[1]:r[2]:r[3]]
+    return T[r[0]][:, r[1]:r[2]]
+
+
+def _count(r):
+    return (r[2] - r[1] + (r[3] - 1 if len(r) == 4 else 0)) // (r[3] if len(r) == 4 else 1)
+
+
+def _psum(name):
+    return SCRATCH[name][0] == "psum" if name in SCRATCH else False
+
+
+def design():
+    ops = []
+
+    def op(eng, f, rd, wr, dur, lat=WAKE, name="", **kw):
+        o = {"eng": eng, "f": f, "rd": [_span(r) for r in rd], "wr": [_span(r) for r in wr], "dur": dur, "lat": lat, "name": name}
+        o.update(kw)
+        ops.append(o)
+
+    def tt(out, a, b, alu, name="tt"):
+        c = 1 if (_psum(a[0]) or _psum(b[0])) else 2
+        op("V", lambda q, T: q.tensor_tensor(_ap(T, out), _ap(T, a), _ap(T, b), alu), [a, b], [out],
+           0.02 + CY * max(64, c * _count(out)), name=name)
+
+    def ts(out, a, s1, s2, op0, op1=None, name="ts"):
+        aps = [s for s in (s1, s2) if isinstance(s, tuple)]
+        two = all(SCRATCH[r[0]][2] in (_B, _U) for r in (out, a))
+
+        def f(q, T):
+            x1 = _ap(T, s1) if isinstance(s1, tuple) else s1
+            x2 = _ap(T, s2) if isinstance(s2, tuple) else s2
+            if op1 is None:
+                return q.tensor_scalar(_ap(T, out), _ap(T, a), x1, None, op0)
+            return q.tensor_scalar(_ap(T, out), _ap(T, a), x1, x2, op0, op1)
+        op("V", f, [a] + aps, [out], 0.02 + CY * max(64, (0.5 if two else 1) * _count(out)), name=name)
+
+    def copy(out, a, name="copy"):
+        op("V", lambda q, T: q.tensor_copy(_ap(T, out), _ap(T, a)), [a], [out], 0.02 + CY * max(64, _count(out)), name=name)
+
+    def memset(buf, lo, hi, val, p0=0, p1=128):
+        op("V", lambda q, T: q.memset(T[buf][p0:p1, lo:hi], val), [], [(buf, lo, hi)], 0.02 + CY * max(64, 0.5 * (hi - lo)), name="memset")
+
+    def gtt(out, win, off, b, alu, name):
+        op("V", lambda q, T: q.tensor_tensor(_ap(T, out), _ap(T, win).indirect(_ap(T, off)), _ap(T, b), alu), [win, off, b], [out],
+           0.05 + CY * GA * _count(out), name=name)
+
+    def gather(out, win, off, name, eng="S"):
+        def f(q, T, e):
+            if e == "V":
+                return q.tensor_copy(_ap(T, out), _ap(T, win).indirect(_ap(T, off)))
+            return q.activation(_ap(T, out), _ap(T, win).indirect(_ap(T, off)), ActivationFunctionType.Copy)
+        op(eng, f, [win, off], [out], 0.06 + CY * GA * _count(out), name=name, flex=True)
+
+    def absS(out, a, name):
+        op("S", lambda q, T: q.activation(_ap(T, out), _ap(T, a), ActivationFunctionType.Abs), [a], [out],
+           0.1 + CY * _count(out), name=name)
+
+    def sub(out, a, b, name):
+        def f(q, T):
+            n = out[2] - out[1]
+            for s in range(0, n, BANK):
+                e = min(n, s + BANK)
+                q.matmul(T[out[0]][:, out[1] + s:out[1] + e], T["ident"][:], T[a[0]][:, a[1] + s:a[1] + e], True, False)
+                i = q.matmul(T[out[0]][:, out[1] + s:out[1] + e], T["nident"][:], T[b[0]][:, b[1] + s:b[1] + e], False, True)
+            return i
+        op("P", f, [a, b, ("ident", 0, 128), ("nident", 0, 128)], [out], PEC * 2 * _count(out), name=name)
+
+    def total(out, a, wb, const, name):
+        def f(q, T):
+            o = _ap(T, out)
+            if const is not None:
+                q.matmul(o, T["ones"][:], T[const[0]][:, const[1]:const[1] + out[2] - out[1]], True, False)
+            for p in range(16):
+                i = q.matmul(o, T[wb][:, 15 - p:143 - p], T[a[0]][:, a[1] + p:a[2]:16], const is None and p == 0, p == 15)
+            return i
+        op("P", f, [a, (wb, 0, 144), ("ones", 0, 128)] + ([(const[0], const[1], const[1] + 64)] if const else []), [out],
+           PEC * 64 * (17 if const else 16), name=name)
+
+    nd = [0]
+
+    def dma(q, fo, fi, rd, wr, name, nbytes=0):
+        k = nd[0]
+        nd[0] += 1
+        op(q, lambda e, T: e.dma_start(fo(T), fi(T)), rd, wr, 0.06, lat=2.0 + nbytes / 200e3, name=name, dma="d%d" % k)
+
+    dma("S", lambda T: T.fl[:, 0:W], lambda T: T.flood[:], [], [("fl", 0, W)], "ld flood", 524288)
+    dma("Y", lambda T: T["rn_0"][:, 0:P], lambda T: T.riv[:], [], [("rn_0", 0, P)], "ld riv", 131072)
+    dma("Y", lambda T: T["mn_0"][:, 0:P], lambda T: T.bord[:], [], [("mn_0", 0, P)], "ld bord", 131072)
+    dma("S", lambda T: T.fl[:, W:2 * W], lambda T: T.flood[:], [], [("fl", W, 2 * W)], "ld flood2", 524288)
+    dma("Y", lambda T: T.thi[:], lambda T: T.th[:], [], [("thi", 0, 1)], "ld th")
+    dma("Y", lambda T: T.epi[:], lambda T: T.eps[:], [], [("epi", 0, 1)], "ld eps")
+    iota = lambda out, pat, base, cm, dtype=_I: op(
+        "G", lambda q, T: q.iota(_ap(T, out), pat, base, cm, allow_small_or_imprecise_dtypes=True) if dtype == _F else q.iota(_ap(T, out), pat, base, cm),
+        [], [out], 0.13 + 2 * CY * _count(out), name="iota")
+
+    def asel(out, a, pat, cmp, base, cm):
+        op("G", lambda q, T: q.affine_select(_ap(T, out), _ap(T, a), pat, cmp, 0.0, base, cm), [a], [out], 0.17 + 2 * CY * _count(out), name="asel")
+
+    memset("ones", 0, 128, 1.0)
+    iota(("ipt", 0, 64), [[0, 64]], 0, 1)
+    iota(("i16", 0, 64), [[16, 64]], 0, 0)
+    asel(("ident", 0, 128), ("ones", 0, 128), [[-1, 128]], OP.is_equal, 0, 1)
+    asel(("g8", 0, 8), ("ones", 0, 8), [[-16, 8]], OP.is_ge, 0, 1)
+    asel(("g8b", 0, 8), ("g8", 0, 8), [[16, 8]], OP.is_ge, 15, -1)
+    iota(("iot", 0, 256), [[1, 256]], 0, 0, _F)
+    iota(("dgi", 0, 512), [[0, 32], [1, 16]], 0, -1)
+    iota(("dgj", 0, 512), [[0, 32], [1, 16]], 0, 0)
+    ts(("nident", 0, 128), ("ident", 0, 128), -1.0, None, OP.mult)
+    memset("b1", 0, 144, 0.0)
+    copy(("b1", 15, 143, 16), ("g8b", 0, 8))
+    for w in (8192, 16384, 4096):
+        ts(("b%d" % w, 0, 144), ("b1", 0, 144), float(w), None, OP.mult)
+    memset("ck", 0, 320, -262144.0, 0, 64)
+    for m in range(4):
+        memset("ck", 64 * m, 64 * m + 64, 32.0 * m, 64, 128)
+    memset("ck", 256, 320, 128.0, 64, 128)
+    cons = [(77 * t - 592) % W for t in range(ROUNDS)]
+    memset("cy", 0, 192, -2176.0, 0, 64)
+    for t in range(ROUNDS):
+        x = cons[t] / 32.0
+        hi = int(x * 4) / 4.0
+        memset("cy", 64 * t, 64 * t + 64, hi, 64, 96)
+        memset("cy", 64 * t, 64 * t + 64, x - hi, 96, 128)
+    memset("cz", 0, 64, -544.0, 0, 64)
+    memset("cz", 0, 64, 0.0, 64, 128)
+    ts(("ip2", 0, 64), ("ipt", 0, 64), 15, None, OP.bitwise_and)
+    tt(("cpos", 0, 64), ("ip2", 0, 64), ("i16", 0, 64), OP.add)
+    POS, IOT = ("pv", 0, 64), ("pv", 64, 128)
+    copy(POS, ("cpos", 0, 64))
+    copy(IOT, ("iot", 0, 64))
+    ts(("cpos", 0, 64), ("cpos", 0, 64), 4096.0, None, OP.add)
+    ts(("dgi", 0, 512), ("dgi", 0, 512), 15, None, OP.bitwise_and)
+    ts(("diag", 0, 512), ("dgi", 0, 512), 0.0, None, OP.is_equal)
+    ts(("seg", 0, 512), ("dgj", 0, 512), 0.0, None, OP.is_gt)
+    copy(("tha", 0, 1), ("thi", 0, 1))
+    copy(("epf", 0, 1), ("epi", 0, 1))
+    for k in range(2):
+        memset("rf_%d" % k, 257, 264, 592.0)
+        memset("mf_%d" % k, 256, 264, 592.0)
+        memset("rp_%d" % k, 256, 296, -4096)
+        memset("xr_%d" % k, 4096, 4112, 0.0)
+
+    FL = ("fl", 0, W)
+    FL2 = ("fl", 0, 2 * W)
+    for lo, hi, e in FIRST:
+        copy(("ru0", lo, hi), ("rn_0", lo, hi), "R u16")
+        gather(("xr_0", 16 * lo, 16 * hi), FL, ("ru0", lo, hi), "XR0", e)
+    ts(("rf_0", 1, 257), ("rn_0", 0, 256), 592.0, None, OP.add)
+    copy(("rf_0", 0, 1), ("rf_0", 1, 2))
+    ts(("mf_0", 0, 256), ("mn_0", 0, 256), 592.0, None, OP.add)
+    for lo, hi in ((0, 64), (64, 128), (128, 192), (192, 256)):
+        copy(("mu_0", lo, hi), ("mn_0", lo, hi), "M u16")
+        gather(("xm", 16 * lo, 16 * hi), FL, ("mu_0", lo, hi), "XM0")
+
+    nkc = [0]
+
+    def nkcol():
+        c = nkc[0]
+        nkc[0] += 1
+        return ("nk", c, c + 1)
+    neck = {}
+
+    def halves(lo, hi, yes):
+        if not yes or hi - lo <= 32:
+            return [(lo, hi)]
+        m = (lo + hi) // 2
+        return [(lo, m), (m, hi)]
+
+    def step1(t, k):
+        s = (4 * t + k) % 2
+        z = t % 2
+        b = lambda n: n + "_%d" % s
+        c0 = CK * k
+        rn, rf, mn, mf = "rn_%d" % z, "rf_%d" % z, "mn_%d" % z, "mf_%d" % z
+        xr = "xr_%d" % z
+        R16, K12, M5, UU = ("pv", 128, 192), ("pv", 192, 320), ("pv", 320, 384), ("pv", 384, 448)
+        T5, ZZ = ("pv", 192, 256), ("pv", 256, 320)
+        xn = (xr, 16 * (c0 + 1), 16 * (c0 + 65))
+        sc = "sc%d" % s
+        ts(R16, (rn, c0, c0 + 64), 16.0, None, OP.add, name="R16")
+        for m, (bf, o) in enumerate(((rf, c0), (rf, c0 + 2), (mf, c0), (mf, c0 + 1))):
+            tt((b("pr"), 64 * m, 64 * m + 64), R16, (bf, o, o + 64), OP.mult, name="prod")
+        for h in range(0, 256, 128):
+            ts((b("v"), h, h + 128), (b("pr"), h, h + 128), 4, W - 1, OP.arith_shift_right, OP.bitwise_and, name="v")
+            ts((b("u"), h, h + 128), (b("v"), h, h + 128), float(cons[t]), None, OP.add, name="u")
+        sub(("sub0", 0, CE), (xr, 16 * c0, 16 * (c0 + 64)), xn, "now-")
+        absS((b("now"), 0, CE), ("sub0", 0, CE), "now||")
+        sub(("sub0", 0, CE), ("xm", 16 * c0, 16 * (c0 + 64)), xn, "c5-")
+        absS((b("win"), 4 * CE, 5 * CE), ("sub0", 0, CE), "c5||")
+        for m in range(4):
+            gtt((b("xd"), CE * m, CE * m + CE), FL2, (b("u"), 64 * m, 64 * m + 64), xn, OP.subtract, "cand")
+            absS((b("win"), CE * m, CE * m + CE), (b("xd"), CE * m, CE * m + CE), "cand||")
+        for m in (4, 0, 1, 2, 3):
+            total((sc, 64 * m, 64 * m + 64), (b("win"), CE * m, CE * m + CE), "b8192", ("ck", 64 * m), "score")
+        tt(K12, (sc, 0, 128), (b("v"), 0, 128), OP.add, "key")
+        tt((b("kb"), 0, 128), (sc, 128, 256), (b("v"), 128, 256), OP.add, "key")
+        tt((b("kc"), 0, 128), K12, (b("kb"), 0, 128), OP.min, "kmin")
+        tt((b("k4"), 0, 64), (b("kc"), 0, 64), (b("kc"), 64, 128), OP.min, "kmin")
+        tt(M5, (sc, 256, 320), (b("k4"), 0, 64), OP.is_le, "m5")
+        ts((b("ka"), 0, 64), (b("k4"), 0, 64), 6144, 1, OP.bitwise_and, OP.arith_shift_right, name="ka")
+        tt(UU, M5, ("cpos", 0, 64), OP.mult, "uu")
+        tt((b("w"), 0, 64), POS, (b("ka"), 0, 64), OP.add, "w")
+        tt((b("o"), 0, 64), UU, (b("w"), 0, 64), OP.max, "o")
+        copy((b("ou"), 0, 64), (b("o"), 0, 64), "ou")
+        gtt((b("nb"), 0, CE), (b("win"), 0, 5 * CE), (b("ou"), 0, 64), (b("now"), 0, CE), OP.is_lt, "nearer")
+        ts((b("kv"), 0, 64), (b("k4"), 0, 64), W - 1, None, OP.bitwise_and, name="kv")
+        ts((b("me"), 0, 64), (mn, c0, c0 + 64), 4096.0 - cons[t], None, OP.add, name="me")
+        tt(T5, M5, (b("me"), 0, 64), OP.mult, "t5")
+        tt((b("d"), 0, 64), T5, (b("kv"), 0, 64), OP.max, "d")
+        total((sc, 320, 384), (b("nb"), 0, CE), "b16384", ("cy", 64 * t), "cnt1")
+        tt(ZZ, (sc, 320, 384), (b("d"), 0, 64), OP.add, "z")
+        tt((b("rr"), 0, 64), ZZ, (rn, c0, c0 + 64), OP.max, "rr")
+        rp, rpu = "rp_%d" % z, "rpu_%d" % z
+        e = 63 if k == 3 else 64
+        ts((rp, c0, c0 + e), (b("rr"), 0, e), W - 1, None, OP.bitwise_and, name="R'")
+        if k == 3:
+            copy((rp, 255, 256), (rn, 255, 256), "R'255")
+        copy((rpu, c0, c0 + 64), (rp, c0, c0 + 64), "R'u")
+        for a, c in halves(c0, c0 + 64, 4 * t + k >= TAIL):
+            gather(("xp", 16 * a, 16 * c), FL, (rpu, a, c), "XR'", "VS" if 4 * t + k >= TAIL else "S")
+
+    def necks(t, k):
+        s = (4 * t + k) % 2
+        b = lambda n: n + "_%d" % s
+        lo, hi = max(0, 64 * k - 32), 64 * k + 32
+        n = hi - lo
+        for a, c in halves(lo, hi, 4 * t + k >= TAIL):
+            h0, h1 = 16 * (a - lo), 16 * (c - lo)
+            sub(("sub1", h0, h1), ("xp", 16 * a, 16 * c), ("xp", 16 * (a + 32), 16 * (c + 32)), "nk-")
+            absS((b("a2"), h0, h1), ("sub1", h0, h1), "nk||")
+        total(("cnt", 0, n), (b("a2"), 0, 16 * n), "b1", None, "dist")
+        ts((b("nf"), 0, n), ("cnt", 0, n), ("tha", t, t + 1), 256.0, OP.is_ge, OP.mult, name="nf")
+        tt((b("q"), 0, n), ("pv", 64, 64 + n), (b("nf"), 0, n), OP.add, "q")
+        m = nkcol()
+        qq = (b("q"), 0, n)
+        op("V", lambda e, T: e.tensor_reduce(_ap(T, m), _ap(T, qq), AxisListType.X, OP.min), [qq], [m], 0.02 + CY * 64, name="red")
+        m2 = nkcol()
+        ts(m2, m, float(lo), 256.0, OP.add, OP.min, name="nk")
+        if k:
+            m3 = nkcol()
+            tt(m3, m2, neck[t, k - 1], OP.min, "nkmin")
+            m2 = m3
+        neck[t, k] = m2
+
+    def loops(t):
+        z = t % 2
+        nk = neck[t, 3]
+        lout = "lout%d" % t
+        ts(("lu", 0, 32), ("iot", 0, 32), nk, 1.0, OP.add, OP.add, name="lu")
+        gtt(("lg", 0, 512), ("rp_%d" % z, 0, 296), ("lu", 0, 32), ("diag", 0, 512), OP.mult, "loop")
+        op("V", lambda e, T: e.tensor_tensor_scan(T.ls[:], T.seg[:], T.lg[:], 0.0, OP.mult, OP.add), [("seg", 0, 512), ("lg", 0, 512)], [("ls", 0, 512)],
+           0.02 + CY * 512, name="scan")
+        copy((lout, 0, 32), ("ls", 15, 512, 16), "lout")
+        op("G", None, [(lout, 0, 32)], [], 1.0, name="send", send=t)
+        op("N", None, [(lout, 0, 32)], [("land%d" % t, 0, 32)], 0.0, lat=7.0, name="recv", recv=t)
+        ts(("tha", 4 + t, 5 + t), nk, 256.0, 16.0, OP.is_lt, OP.mult, name="A")
+        tt(("tha", t + 1, t + 2), ("tha", t, t + 1), ("tha", 4 + t, 5 + t), OP.add, "A")
+
+    def landed(t):
+        ts(("l1", 0, 32), ("land%d" % t, 0, 32), 0.0, -8192.0, OP.is_ge, OP.mult, name="l1")
+        tt(("l1", 0, 32), ("l1", 0, 32), ("lout%d" % t, 0, 32), OP.add, "l1")
+        tt(("l2", 0, 32), ("l1", 0, 32), ("land%d" % t, 0, 32), OP.max, "l2")
+
+    def moved(t, k):
+        s = (4 * t + k) % 2
+        b = lambda n: n + "_%d" % s
+        z, y = t % 2, (t + 1) % 2
+        last = t == ROUNDS - 1
+        lo, hi = (max(0, 64 * k - 32), 64 * k + 32) if k < 4 else (224, 256)
+        n = hi - lo
+        rp = "rp_%d" % z
+        rn = ("yrf", lo, hi) if last else ("rn_%d" % y, lo, hi)
+        src = (rp, lo + 32, hi + 32) if k < 4 else ("l2", 0, 32)
+        MK = ("pv", 448, 448 + n)
+        tt((b("df"), 0, n), src, (rp, lo, hi), OP.subtract, "df")
+        ts(MK, ("iot", lo, hi), neck[t, min(k, 3)], None, OP.is_gt, name="mk")
+        tt(MK, MK, (b("df"), 0, n), OP.mult, "dm")
+        tt(rn, MK, (rp, lo, hi), OP.add, "R''")
+        u = ("r2u_%d" % z, lo, hi)
+        copy(u, rn, "R''u")
+        tail = 4 * t + k >= TAIL
+        for a, c in halves(lo, hi, tail):
+            gather(("xr_%d" % y, 16 * a, 16 * c), FL, ("r2u_%d" % z, a, c), "XR''", "VS" if tail else "S")
+        if not last:
+            rf = "rf_%d" % y
+            ts((rf, lo + 1, hi + 1), rn, 592.0, None, OP.add, name="rf")
+            if k == 0:
+                copy((rf, 0, 1), (rf, 1, 2), "rf0")
+        for a, c in halves(lo, hi, tail):
+            h0, h1 = 16 * (a - lo), 16 * (c - lo)
+            sub(("sub1", h0, h1), ("xr_%d" % y, 16 * a, 16 * c), ("xm", 16 * a, 16 * c), "ac-")
+            absS((b("a3"), h0, h1), ("sub1", h0, h1), "ac||")
+            ts((b("c3"), h0, h1), (b("a3"), h0, h1), ("epf", 0, 1), None, OP.is_le, name="c3")
+        total(("cnt", 64, 64 + n), (b("c3"), 0, 16 * n), "b4096", ("cz", 0), "cnt3")
+        Z3 = ("pv", 448, 448 + n)
+        tt(Z3, ("cnt", 64, 64 + n), rn, OP.add, "z3")
+        tt((b("mm"), 0, n), Z3, ("mn_%d" % z, lo, hi), OP.max, "mm")
+        mn = ("mn_%d" % y, lo, hi)
+        ts(mn, (b("mm"), 0, n), W - 1, None, OP.bitwise_and, name="M'")
+        if last:
+            copy(("ymf", lo, hi), mn, "M f")
+            return
+        ts(("mf_%d" % y, lo, hi), mn, 592.0, None, OP.add, name="mf")
+        mu = ("mu_%d" % y, lo, hi)
+        copy(mu, mn, "M'u")
+        gather(("xm", 16 * lo, 16 * hi), FL, mu, "XM'")
+
+    for slot in range(4 * ROUNDS + 3):
+        if slot < 4 * ROUNDS:
+            step1(slot // 4, slot % 4)
+        e = slot - 1
+        if 0 <= e < 4 * ROUNDS:
+            t, k = divmod(e, 4)
+            necks(t, k)
+            if k == 3:
+                loops(t)
+            moved(t, k)
+        f = slot - 2
+        if f >= 0 and f % 4 == 3 and f < 4 * ROUNDS:
+            landed(f // 4)
+            moved(f // 4, 4)
+    tt(("aout", 0, 1), ("tha", ROUNDS, ROUNDS + 1), ("tha", 0, 1), OP.subtract)
+    ts(("aout", 1, 2), ("aout", 0, 1), 0.0625, None, OP.mult)
+    dma("Y", lambda T: T.ya[:], lambda T: T.aout[:, 1:2], [("aout", 1, 2)], [], "st ya")
+    dma("Y", lambda T: T.yr[:, 0:224], lambda T: T.yrf[:, 0:224], [("yrf", 0, 224)], [], "st yr")
+    dma("Y", lambda T: T.ym[:, 0:224], lambda T: T.ymf[:, 0:224], [("ymf", 0, 224)], [], "st ym")
+    dma("Y", lambda T: T.yr[:, 224:256], lambda T: T.yrf[:, 224:256], [("yrf", 224, 256)], [], "st yr")
+    dma("Y", lambda T: T.ym[:, 224:256], lambda T: T.ymf[:, 224:256], [("ymf", 224, 256)], [], "st ym")
+    return ops
+
+
+def depend(ops):
+    acc = {}
+    for i, o in enumerate(ops):
+        dep = set()
+        touches = [(r, False) for r in o["rd"]] + [(r, True) for r in o["wr"]]
+        for (buf, lo, hi), wr in touches:
+            lst = acc.setdefault(buf, [])
+            ps = _psum(buf)
+            for (j, l2, h2, w2) in lst:
+                if j == i:
+                    continue
+                hit = lo < h2 and l2 < hi and (wr or w2)
+                if ps and not hit:
+                    hit = ops[j]["eng"] != o["eng"] and lo // BANK <= (h2 - 1) // BANK and l2 // BANK <= (hi - 1) // BANK
+                if hit:
+                    dep.add(j)
+        for (buf, lo, hi), wr in touches:
+            lst = acc[buf]
+            if wr and not _psum(buf):
+                lst[:] = [a for a in lst if not (lo <= a[1] and a[2] <= hi)]
+            lst.append((i, lo, hi, wr))
+        o["dep"] = dep
+
+
+def arrange(ops):
+    n = len(ops)
+    succ = [[] for _ in range(n)]
+    for i, o in enumerate(ops):
+        for j in o["dep"]:
+            succ[j].append(i)
+    rank = [0.0] * n
+    for i in range(n - 1, -1, -1):
+        o = ops[i]
+        rank[i] = o["dur"] + o["lat"] + max([rank[j] for j in succ[i]], default=0.0)
+    left = [len(o["dep"]) for o in ops]
+    at = [0.0] * n
+    free = {"V": 0.0, "S": 0.0, "P": 0.0, "G": 0.0, "Y": 0.0, "N": 0.0}
+    ready = {e: [] for e in free}
+
+    def push(i):
+        for e in ops[i]["eng"]:
+            ready[e].append(i)
+    for i in range(n):
+        if not left[i]:
+            push(i)
+    order = {e: [] for e in free}
+    done = 0
+    end = 0.0
+    while done < n:
+        best = None
+        for e in free:
+            if ready[e]:
+                t = max(free[e], min(at[i] for i in ready[e]))
+                if best is None or t < best[0]:
+                    best = (t, e)
+        t, e = best
+        i = max((j for j in ready[e] if at[j] <= t), key=lambda j: (rank[j], -j))
+        o = ops[i]
+        for x in o["eng"]:
+            ready[x].remove(i)
+        o["on"] = e
+        o["t0"] = t
+        order[e].append(i)
+        free[e] = t + o["dur"] if e != "N" else 0.0
+        f = t + o["dur"] + o["lat"]
+        end = max(end, f)
+        done += 1
+        for j in succ[i]:
+            at[j] = max(at[j], f)
+            left[j] -= 1
+            if not left[j]:
+                push(j)
+    return order, end
+
+
+_made = {}
+
+
+def made():
+    if not _made:
+        ops = design()
+        depend(ops)
+        order, end = arrange(ops)
+        _made["ops"], _made["order"], _made["end"] = ops, order, end
+        num = {}
+        for e in "VSPG":
+            c = 0
+            for i in order[e]:
+                if "dma" in ops[i] or "send" in ops[i]:
+                    continue
+                c += 1
+                num[i] = c
+        _made["num"] = num
+        seq = sorted(range(len(ops)), key=lambda i: (ops[i]["t0"], i))
+        pos = {i: n for e in order for n, i in enumerate(order[e])}
+        state = {e: {} for e in order}
+        after = {}
+        waits = {}
+        todo = {e: 0 for e in order}
+        ndone = 0
+        while ndone < len(seq):
+            for e in order:
+                while todo[e] < len(order[e]) and all(j in after for j in ops[order[e][todo[e]]]["dep"]):
+                    i = order[e][todo[e]]
+                    o = ops[i]
+                    st = state[e] if e != "N" else {}
+                    need = {}
+                    for j in o["dep"]:
+                        key, val = _key(j, ops, num)
+                        if key is not None and st.get(key, 0) < val and need.get(key, (0, 0))[0] < val:
+                            need[key] = (val, j)
+                    out = []
+                    for key, (val, j) in sorted(need.items(), key=lambda kv: -pos[kv[1][1]]):
+                        if st.get(key, 0) >= val:
+                            continue
+                        out.append((key, val))
+                        for a, c in after[j].items():
+                            st[a] = max(st.get(a, 0), c)
+                        st[key] = max(st.get(key, 0), val)
+                    waits[i] = out
+                    me = dict(st)
+                    key, val = _key(i, ops, num)
+                    if key is not None:
+                        me[key] = val
+                    after[i] = me
+                    todo[e] += 1
+                    ndone += 1
+        _made["waits"] = waits
+    return _made
+
+
+def _key(i, ops, num):
+    o = ops[i]
+    if "dma" in o:
+        return o["dma"], 16
+    if "send" in o:
+        return None, 0
+    if "recv" in o:
+        return "arr%d" % o["recv"], 8
+    return "s" + o["on"], num[i]
+
+
+def rank_program(g, core, T, topo):
+    rank = T.rank_of(core)
+    if rank is None:
+        return
+    m = made()
+    ops, order, waits = m["ops"], m["order"], m["waits"]
+    queues = {"V": g.vector, "S": g.scalar, "P": g.tensor, "G": g, "Y": g.sync}
+    sent = 0
+    for e in ("G", "Y", "S", "V", "P"):
+        q = queues[e]
+        for i in order[e]:
+            o = ops[i]
+            for key, val in waits[i]:
+                q.wait_ge(T.sem[key], val)
+            if "send" in o:
+                t = o["send"]
+                dst = T.cores[(rank + 1 + t % (N - 1)) % N]
+                rid, pid, _ = topo.addr(dst)
+                eng = topo.engines(core, dst)[:8]
+                g.remote_dma(out_ap=T["land%d" % t][:], in_ap=T["lout%d" % t][:], remote_sem=T.sem["arr%d" % t], local_sem=T.sem.ls,
+                             pid=pid, routing_id=rid, dma_engine_mask=sum(1 << x for x in eng))
+                sent += len(eng)
+            elif "dma" in o:
+                o["f"](q, T).then_inc(T.sem[o["dma"]], 16)
+            elif "flex" in o:
+                o["f"](q, T, e).then_inc(T.sem["s" + e], 1)
+            else:
+                o["f"](q, T).then_inc(T.sem["s" + e], 1)
+    g.wait_ge(T.sem.ls, sent)
+    for i, o in enumerate(ops):
+        if "dma" in o and o["name"].startswith("st"):
+            g.sync.wait_ge(T.sem[o["dma"]], 16)
+    for e in "VSPG":
+        g.sync.wait_ge(T.sem["s" + e], max(c for i, c in m["num"].items() if ops[i]["on"] == e))

@@ -4,6 +4,7 @@ from concourse.mybir import dt, AluOpType, AxisListType, ActivationFunctionType
 OP = AluOpType
 N, W, P, L, ROUNDS = 8, 2048, 256, 32, 3
 CK = 64
+FW = 1616
 CE = 16 * CK
 BANK = 512
 
@@ -15,15 +16,15 @@ SCRATCH = {
     "g8": ("sbuf", [128, 8], _B), "g8b": ("sbuf", [128, 8], _B),
     "b1": ("sbuf", [128, 144], _B), "b4096": ("sbuf", [128, 144], _B),
     "b8192": ("sbuf", [128, 144], _B), "b16384": ("sbuf", [128, 144], _B),
-    "ck": ("sbuf", [128, 320], _B), "cy": ("sbuf", [128, 192], _B), "cz": ("sbuf", [128, 64], _B),
+    "ck": ("sbuf", [128, 320], _B), "cy": ("sbuf", [128, 192], _B), "cz": ("sbuf", [128, 128], _B),
     "iot": ("sbuf", [128, 256], _F), "i16": ("sbuf", [128, 64], _I), "ipt": ("sbuf", [128, 64], _I),
     "ip2": ("sbuf", [128, 64], _I), "cpos": ("sbuf", [128, 64], _F),
     "dgi": ("sbuf", [128, 512], _I), "dgj": ("sbuf", [128, 512], _I), "diag": ("sbuf", [128, 512], _F), "seg": ("sbuf", [128, 512], _F),
-    "thi": ("sbuf", [128, 1], _I), "epi": ("sbuf", [128, 1], _I), "epf": ("sbuf", [128, 1], _F),
+    "thi": ("sbuf", [128, 1], _I), "epi": ("sbuf", [128, 1], _I), "epf": ("sbuf", [128, 2], _F),
     "tha": ("sbuf", [128, 8], _F), "nk": ("sbuf", [128, 64], _F), "aout": ("sbuf", [128, 4], _F),
     "ru0": ("sbuf", [128, 256], _U), "lu": ("sbuf", [128, 32], _U),
     "lg": ("sbuf", [128, 512], _F), "ls": ("sbuf", [128, 512], _F),
-    "l1": ("sbuf", [128, 32], _F), "l2": ("sbuf", [128, 32], _F),
+    "l1": ("sbuf", [128, 32], _F), "lm": ("sbuf", [128, 32], _F), "lo": ("sbuf", [128, 32], _F), "l2": ("sbuf", [128, 32], _F),
     "yrf": ("sbuf", [128, 256], _F), "ymf": ("sbuf", [128, 256], _F),
     "pv": ("psum", [128, 512], _F), "sc0": ("psum", [128, 512], _F), "sc1": ("psum", [128, 512], _F),
     "cnt": ("psum", [128, 512], _F), "sub0": ("psum", [128, 1024], _F), "sub1": ("psum", [128, 1024], _F),
@@ -42,11 +43,18 @@ for _k in range(2):
 NDMA = 16
 SEMAPHORES = ["sV", "sS", "sP", "sG", "ls", "arr0", "arr1", "arr2"] + ["d%d" % k for k in range(NDMA)]
 
-CY = 0.00083 * 1.2
-GA = 1.5
-PEC = 0.0005
-WAKE = 0.06
-TAIL = 4 * ROUNDS - 2
+CY = 0.000833
+GA = 1.47
+PEC = 0.00053
+WAKE = 0.069
+BONUS = {"nearer": 4.0, "loop": -3.2, "score": -7.1, "nk-": -5.2, "now||": -1.0, "cnt3": 5.2, "XM'": -0.3, "ac||": 0.1, "now-": 0.9,
+         "nk||": 3.4, "ac-": -2.2, "df": -0.6, "c5||": 0.9, "c3": -0.3, "rf": 5.4, "cand||": 0.1, "u": 2.1, "XR'": -1.2, "me": -0.8,
+         "cand": 1.0, "c5-": -1.6, "v": -1.8, "dist": -0.1, "kmin": 3.7}
+VIAS = (0, 1, 2, 3)
+VW = 128
+NET = 5.5
+XMV = "SSSSSSSSSS"
+TAIL = 4 * ROUNDS - 1
 FIRST = ((0, 66, "S"), (66, 130, "V"), (130, 194, "S"), (194, 256, "S"))
 
 
@@ -124,16 +132,17 @@ def design():
             return i
         op("P", f, [a, b, ("ident", 0, 128), ("nident", 0, 128)], [out], PEC * 2 * _count(out), name=name)
 
-    def total(out, a, wb, const, name):
+    def total(out, a, wb, const, name, *more):
         def f(q, T):
             o = _ap(T, out)
             if const is not None:
                 q.matmul(o, T["ones"][:], T[const[0]][:, const[1]:const[1] + out[2] - out[1]], True, False)
-            for p in range(16):
-                i = q.matmul(o, T[wb][:, 15 - p:143 - p], T[a[0]][:, a[1] + p:a[2]:16], const is None and p == 0, p == 15)
+            todo = [(x, p) for x in (a,) + more for p in range(16)]
+            for n, (x, p) in enumerate(todo):
+                i = q.matmul(o, T[wb][:, 15 - p:143 - p], T[x[0]][:, x[1] + p:x[2]:16], const is None and n == 0, n == len(todo) - 1)
             return i
-        op("P", f, [a, (wb, 0, 144), ("ones", 0, 128)] + ([(const[0], const[1], const[1] + 64)] if const else []), [out],
-           PEC * 64 * (17 if const else 16), name=name)
+        op("P", f, [a, (wb, 0, 144), ("ones", 0, 128)] + list(more) + ([(const[0], const[1], const[1] + 64)] if const else []), [out],
+           PEC * 64 * (16 * (1 + len(more)) + (1 if const else 0)), name=name)
 
     nd = [0]
 
@@ -145,9 +154,9 @@ def design():
     dma("S", lambda T: T.fl[:, 0:W], lambda T: T.flood[:], [], [("fl", 0, W)], "ld flood", 524288)
     dma("Y", lambda T: T["rn_0"][:, 0:P], lambda T: T.riv[:], [], [("rn_0", 0, P)], "ld riv", 131072)
     dma("Y", lambda T: T["mn_0"][:, 0:P], lambda T: T.bord[:], [], [("mn_0", 0, P)], "ld bord", 131072)
-    dma("S", lambda T: T.fl[:, W:2 * W], lambda T: T.flood[:], [], [("fl", W, 2 * W)], "ld flood2", 524288)
     dma("Y", lambda T: T.thi[:], lambda T: T.th[:], [], [("thi", 0, 1)], "ld th")
     dma("Y", lambda T: T.epi[:], lambda T: T.eps[:], [], [("epi", 0, 1)], "ld eps")
+    dma("S", lambda T: T.fl[:, W:W + FW], lambda T: T.flood[:, 0:FW], [], [("fl", W, W + FW)], "ld flood2", 414000)
     iota = lambda out, pat, base, cm, dtype=_I: op(
         "G", lambda q, T: q.iota(_ap(T, out), pat, base, cm, allow_small_or_imprecise_dtypes=True) if dtype == _F else q.iota(_ap(T, out), pat, base, cm),
         [], [out], 0.13 + 2 * CY * _count(out), name="iota")
@@ -181,7 +190,8 @@ def design():
         memset("cy", 64 * t, 64 * t + 64, hi, 64, 96)
         memset("cy", 64 * t, 64 * t + 64, x - hi, 96, 128)
     memset("cz", 0, 64, -544.0, 0, 64)
-    memset("cz", 0, 64, 0.0, 64, 128)
+    memset("cz", 64, 128, -1568.0, 0, 64)
+    memset("cz", 0, 128, 0.0, 64, 128)
     ts(("ip2", 0, 64), ("ipt", 0, 64), 15, None, OP.bitwise_and)
     tt(("cpos", 0, 64), ("ip2", 0, 64), ("i16", 0, 64), OP.add)
     POS, IOT = ("pv", 0, 64), ("pv", 64, 128)
@@ -193,6 +203,7 @@ def design():
     ts(("seg", 0, 512), ("dgj", 0, 512), 0.0, None, OP.is_gt)
     copy(("tha", 0, 1), ("thi", 0, 1))
     copy(("epf", 0, 1), ("epi", 0, 1))
+    ts(("epf", 1, 2), ("epi", 0, 1), -1.0, None, OP.mult)
     for k in range(2):
         memset("rf_%d" % k, 257, 264, 592.0)
         memset("mf_%d" % k, 256, 264, 592.0)
@@ -200,7 +211,7 @@ def design():
         memset("xr_%d" % k, 4096, 4112, 0.0)
 
     FL = ("fl", 0, W)
-    FL2 = ("fl", 0, 2 * W)
+    FL2 = ("fl", 0, W + FW)
     for lo, hi, e in FIRST:
         copy(("ru0", lo, hi), ("rn_0", lo, hi), "R u16")
         gather(("xr_0", 16 * lo, 16 * hi), FL, ("ru0", lo, hi), "XR0", e)
@@ -233,15 +244,15 @@ def design():
         rn, rf, mn, mf = "rn_%d" % z, "rf_%d" % z, "mn_%d" % z, "mf_%d" % z
         xr = "xr_%d" % z
         R16, K12, M5, UU = ("pv", 128, 192), ("pv", 192, 320), ("pv", 320, 384), ("pv", 384, 448)
-        T5, ZZ = ("pv", 192, 256), ("pv", 256, 320)
+        T5, ZZ, K2 = ("pv", 192, 256), ("pv", 256, 320), ("pv", 256, 320)
         xn = (xr, 16 * (c0 + 1), 16 * (c0 + 65))
         sc = "sc%d" % s
         ts(R16, (rn, c0, c0 + 64), 16.0, None, OP.add, name="R16")
         for m, (bf, o) in enumerate(((rf, c0), (rf, c0 + 2), (mf, c0), (mf, c0 + 1))):
             tt((b("pr"), 64 * m, 64 * m + 64), R16, (bf, o, o + 64), OP.mult, name="prod")
-        for h in range(0, 256, 128):
-            ts((b("v"), h, h + 128), (b("pr"), h, h + 128), 4, W - 1, OP.arith_shift_right, OP.bitwise_and, name="v")
-            ts((b("u"), h, h + 128), (b("v"), h, h + 128), float(cons[t]), None, OP.add, name="u")
+        for h in range(0, 256, VW):
+            ts((b("v"), h, h + VW), (b("pr"), h, h + VW), 4, W - 1, OP.arith_shift_right, OP.bitwise_and, name="v")
+            ts((b("u"), h, h + VW), (b("v"), h, h + VW), float(cons[t]), None, OP.add, name="u")
         sub(("sub0", 0, CE), (xr, 16 * c0, 16 * (c0 + 64)), xn, "now-")
         absS((b("now"), 0, CE), ("sub0", 0, CE), "now||")
         sub(("sub0", 0, CE), ("xm", 16 * c0, 16 * (c0 + 64)), xn, "c5-")
@@ -253,8 +264,9 @@ def design():
             total((sc, 64 * m, 64 * m + 64), (b("win"), CE * m, CE * m + CE), "b8192", ("ck", 64 * m), "score")
         tt(K12, (sc, 0, 128), (b("v"), 0, 128), OP.add, "key")
         tt((b("kb"), 0, 128), (sc, 128, 256), (b("v"), 128, 256), OP.add, "key")
-        tt((b("kc"), 0, 128), K12, (b("kb"), 0, 128), OP.min, "kmin")
-        tt((b("k4"), 0, 64), (b("kc"), 0, 64), (b("kc"), 64, 128), OP.min, "kmin")
+        tt((b("kc"), 0, 64), ("pv", 192, 256), (b("kb"), 0, 64), OP.min, "kmin")
+        tt(K2, K2, (b("kb"), 64, 128), OP.min, "kmin")
+        tt((b("k4"), 0, 64), K2, (b("kc"), 0, 64), OP.min, "kmin")
         tt(M5, (sc, 256, 320), (b("k4"), 0, 64), OP.is_le, "m5")
         ts((b("ka"), 0, 64), (b("k4"), 0, 64), 6144, 1, OP.bitwise_and, OP.arith_shift_right, name="ka")
         tt(UU, M5, ("cpos", 0, 64), OP.mult, "uu")
@@ -294,11 +306,7 @@ def design():
         qq = (b("q"), 0, n)
         op("V", lambda e, T: e.tensor_reduce(_ap(T, m), _ap(T, qq), AxisListType.X, OP.min), [qq], [m], 0.02 + CY * 64, name="red")
         m2 = nkcol()
-        ts(m2, m, float(lo), 256.0, OP.add, OP.min, name="nk")
-        if k:
-            m3 = nkcol()
-            tt(m3, m2, neck[t, k - 1], OP.min, "nkmin")
-            m2 = m3
+        ts(m2, m, float(lo), neck[t, k - 1] if k else 256.0, OP.add, OP.min, name="nk")
         neck[t, k] = m2
 
     def loops(t):
@@ -311,48 +319,67 @@ def design():
            0.02 + CY * 512, name="scan")
         copy((lout, 0, 32), ("ls", 15, 512, 16), "lout")
         op("G", None, [(lout, 0, 32)], [], 1.0, name="send", send=t)
-        op("N", None, [(lout, 0, 32)], [("land%d" % t, 0, 32)], 0.0, lat=7.0, name="recv", recv=t)
+        op("N", None, [(lout, 0, 32)], [("land%d" % t, 0, 32)], 0.0, lat=NET, name="recv", recv=t)
         ts(("tha", 4 + t, 5 + t), nk, 256.0, 16.0, OP.is_lt, OP.mult, name="A")
         tt(("tha", t + 1, t + 2), ("tha", t, t + 1), ("tha", 4 + t, 5 + t), OP.add, "A")
 
     def landed(t):
-        ts(("l1", 0, 32), ("land%d" % t, 0, 32), 0.0, -8192.0, OP.is_ge, OP.mult, name="l1")
-        tt(("l1", 0, 32), ("l1", 0, 32), ("lout%d" % t, 0, 32), OP.add, "l1")
-        tt(("l2", 0, 32), ("l1", 0, 32), ("land%d" % t, 0, 32), OP.max, "l2")
+        rp, lout = ("rp_%d" % (t % 2), 224, 256), ("lout%d" % t, 0, 32)
+        ts(("lm", 0, 32), ("iot", 224, 256), neck[t, 3], None, OP.is_gt, name="l0")
+        tt(("lo", 0, 32), lout, rp, OP.subtract, "l0")
+        tt(("lo", 0, 32), ("lo", 0, 32), ("lm", 0, 32), OP.mult, "l0")
+        tt(("lo", 0, 32), ("lo", 0, 32), rp, OP.add, "l0")
+        ts(("lm", 0, 32), ("lm", 0, 32), 1.0, 8192.0, OP.subtract, OP.mult, name="l0")
+        tt(("l1", 0, 32), ("land%d" % t, 0, 32), ("lm", 0, 32), OP.add, "l1")
+        ts(("l2", 0, 32), ("l1", 0, 32), 0.0, -8192.0, OP.is_ge, OP.mult, name="l1")
+        tt(("l2", 0, 32), ("l2", 0, 32), ("lo", 0, 32), OP.add, "l2")
 
     def moved(t, k):
         s = (4 * t + k) % 2
         b = lambda n: n + "_%d" % s
         z, y = t % 2, (t + 1) % 2
         last = t == ROUNDS - 1
+        cn, c0 = ("sc0", 0) if last and k < 4 else ("cnt", 64)
         lo, hi = (max(0, 64 * k - 32), 64 * k + 32) if k < 4 else (224, 256)
         n = hi - lo
         rp = "rp_%d" % z
         rn = ("yrf", lo, hi) if last else ("rn_%d" % y, lo, hi)
-        src = (rp, lo + 32, hi + 32) if k < 4 else ("l2", 0, 32)
         MK = ("pv", 448, 448 + n)
-        tt((b("df"), 0, n), src, (rp, lo, hi), OP.subtract, "df")
-        ts(MK, ("iot", lo, hi), neck[t, min(k, 3)], None, OP.is_gt, name="mk")
-        tt(MK, MK, (b("df"), 0, n), OP.mult, "dm")
-        tt(rn, MK, (rp, lo, hi), OP.add, "R''")
+        if k < 4:
+            tt((b("df"), 0, n), (rp, lo + 32, hi + 32), (rp, lo, hi), OP.subtract, "df")
+            ts(MK, ("iot", lo, hi), neck[t, k], None, OP.is_gt, name="mk")
+            tt(MK, MK, (b("df"), 0, n), OP.mult, "dm")
+            tt(rn, MK, (rp, lo, hi), OP.add, "R''")
+        else:
+            tt(rn, ("l2", 0, 32), ("l1", 0, 32), OP.max, "R''")
         u = ("r2u_%d" % z, lo, hi)
         copy(u, rn, "R''u")
-        tail = 4 * t + k >= TAIL
-        for a, c in halves(lo, hi, tail):
-            gather(("xr_%d" % y, 16 * a, 16 * c), FL, ("r2u_%d" % z, a, c), "XR''", "VS" if tail else "S")
+        if last and k in VIAS:
+            x = ("xr_%d" % y, 16 * lo, 16 * hi)
+            gather(x, FL, u, "XR''")
+            sub(("sub0", 0, 16 * n), x, ("xm", 16 * lo, 16 * hi), "ac-")
+            absS((b("a3"), 0, 16 * n), ("sub0", 0, 16 * n), "ac||")
+            ts((b("c3"), 0, 16 * n), (b("a3"), 0, 16 * n), ("epf", 0, 1), None, OP.is_le, name="c3")
+            total((cn, c0, c0 + n), (b("c3"), 0, 16 * n), "b4096", ("cz", 0), "cnt3")
+        elif last:
+            x3, c3, c4 = (b("a3"), 0, 16 * n), (b("c3"), 0, 16 * n), (b("nb"), 0, 16 * n)
+            gtt(x3, FL, u, ("xm", 16 * lo, 16 * hi), OP.subtract, "cand")
+            ts(c3, x3, ("epf", 0, 1), None, OP.is_le, name="c3")
+            ts(c4, x3, ("epf", 1, 2), None, OP.is_ge, name="c3")
+            total((cn, c0, c0 + n), c3, "b4096", ("cz", 64), "cnt3", c4)
+        else:
+            gather(("xr_%d" % y, 16 * lo, 16 * hi), FL, u, "XR''")
         if not last:
             rf = "rf_%d" % y
             ts((rf, lo + 1, hi + 1), rn, 592.0, None, OP.add, name="rf")
             if k == 0:
                 copy((rf, 0, 1), (rf, 1, 2), "rf0")
-        for a, c in halves(lo, hi, tail):
-            h0, h1 = 16 * (a - lo), 16 * (c - lo)
-            sub(("sub1", h0, h1), ("xr_%d" % y, 16 * a, 16 * c), ("xm", 16 * a, 16 * c), "ac-")
-            absS((b("a3"), h0, h1), ("sub1", h0, h1), "ac||")
-            ts((b("c3"), h0, h1), (b("a3"), h0, h1), ("epf", 0, 1), None, OP.is_le, name="c3")
-        total(("cnt", 64, 64 + n), (b("c3"), 0, 16 * n), "b4096", ("cz", 0), "cnt3")
+            sub(("sub1", 0, 16 * n), ("xr_%d" % y, 16 * lo, 16 * hi), ("xm", 16 * lo, 16 * hi), "ac-")
+            absS((b("a3"), 0, 16 * n), ("sub1", 0, 16 * n), "ac||")
+            ts((b("c3"), 0, 16 * n), (b("a3"), 0, 16 * n), ("epf", 0, 1), None, OP.is_le, name="c3")
+            total((cn, c0, c0 + n), (b("c3"), 0, 16 * n), "b4096", ("cz", 0), "cnt3")
         Z3 = ("pv", 448, 448 + n)
-        tt(Z3, ("cnt", 64, 64 + n), rn, OP.add, "z3")
+        tt(Z3, (cn, c0, c0 + n), rn, OP.add, "z3")
         tt((b("mm"), 0, n), Z3, ("mn_%d" % z, lo, hi), OP.max, "mm")
         mn = ("mn_%d" % y, lo, hi)
         ts(mn, (b("mm"), 0, n), W - 1, None, OP.bitwise_and, name="M'")
@@ -362,7 +389,7 @@ def design():
         ts(("mf_%d" % y, lo, hi), mn, 592.0, None, OP.add, name="mf")
         mu = ("mu_%d" % y, lo, hi)
         copy(mu, mn, "M'u")
-        gather(("xm", 16 * lo, 16 * hi), FL, mu, "XM'")
+        gather(("xm", 16 * lo, 16 * hi), FL, mu, "XM'", XMV[5 * t + k])
 
     for slot in range(4 * ROUNDS + 3):
         if slot < 4 * ROUNDS:
@@ -373,7 +400,11 @@ def design():
             necks(t, k)
             if k == 3:
                 loops(t)
-            moved(t, k)
+            if t < ROUNDS - 1:
+                moved(t, k)
+            elif k == 3:
+                for j in range(4):
+                    moved(t, j)
         f = slot - 2
         if f >= 0 and f % 4 == 3 and f < 4 * ROUNDS:
             landed(f // 4)
@@ -422,6 +453,8 @@ def arrange(ops):
     for i in range(n - 1, -1, -1):
         o = ops[i]
         rank[i] = o["dur"] + o["lat"] + max([rank[j] for j in succ[i]], default=0.0)
+    for i, o in enumerate(ops):
+        rank[i] += BONUS.get(o["name"], 0.0)
     left = [len(o["dep"]) for o in ops]
     at = [0.0] * n
     free = {"V": 0.0, "S": 0.0, "P": 0.0, "G": 0.0, "Y": 0.0, "N": 0.0}

import numpy as np
from concourse.mybir import dt, AluOpType, AxisListType, ActivationFunctionType

OP = AluOpType
N, W, P, L, ROUNDS = 8, 2048, 256, 32, 3
CK = 64
FW = 1616
CE = 16 * CK
BANK = 512

_F, _B, _I, _U = "float32", "bfloat16", "int32", "uint16"
SCRATCH = {
    "fl": ("sbuf", [128, 2 * W], _B),
    "xm": ("sbuf", [128, 4096], _B), "xp": ("sbuf", [128, 4096], _B),
    "ones": ("sbuf", [128, 128], _B), "ident": ("sbuf", [128, 128], _B), "nident": ("sbuf", [128, 128], _B),
    "g8": ("sbuf", [128, 8], _B), "g8b": ("sbuf", [128, 8], _B),
    "b1": ("sbuf", [128, 144], _B), "b4096": ("sbuf", [128, 144], _B),
    "b8192": ("sbuf", [128, 144], _B), "b16384": ("sbuf", [128, 144], _B),
    "ck": ("sbuf", [128, 320], _B), "cy": ("sbuf", [128, 192], _B), "cz": ("sbuf", [128, 128], _B),
    "iot": ("sbuf", [128, 256], _F), "i16": ("sbuf", [128, 64], _I), "ipt": ("sbuf", [128, 64], _I),
    "ip2": ("sbuf", [128, 64], _I), "cpos": ("sbuf", [128, 64], _F),
    "dgi": ("sbuf", [128, 512], _I), "dgj": ("sbuf", [128, 512], _I), "diag": ("sbuf", [128, 512], _F), "seg": ("sbuf", [128, 512], _F),
    "thi": ("sbuf", [128, 1], _I), "epi": ("sbuf", [128, 1], _I), "epf": ("sbuf", [128, 2], _F),
    "tha": ("sbuf", [128, 8], _F), "nk": ("sbuf", [128, 64], _F), "aout": ("sbuf", [128, 4], _F),
    "ru0": ("sbuf", [128, 256], _U), "lu": ("sbuf", [128, 32], _U),
    "lg": ("sbuf", [128, 512], _F), "ls": ("sbuf", [128, 512], _F),
    "l1": ("sbuf", [128, 32], _F), "lm": ("sbuf", [128, 32], _F), "lo": ("sbuf", [128, 32], _F), "l2": ("sbuf", [128, 32], _F),
    "yrf": ("sbuf", [128, 256], _F), "ymf": ("sbuf", [128, 256], _F),
    "pv": ("psum", [128, 512], _F), "sc0": ("psum", [128, 512], _F), "sc1": ("psum", [128, 512], _F),
    "cnt": ("psum", [128, 512], _F), "sub0": ("psum", [128, 1024], _F), "sub1": ("psum", [128, 1024], _F),
}
for _k in range(3):
    SCRATCH["lout%d" % _k] = ("sbuf", [128, 32], _F)
    SCRATCH["land%d" % _k] = ("sbuf", [128, 32], _F)
for _k in range(2):
    for _n, _c, _d in (("rn", 264, _I), ("rf", 264, _F), ("mn", 264, _I), ("mf", 264, _F), ("rp", 296, _I),
                       ("rpu", 256, _U), ("r2u", 256, _U), ("mu", 256, _U), ("xr", 4112, _B),
                       ("me", 64, _F), ("pr", 256, _I), ("v", 256, _I), ("u", 256, _U), ("xd", 4096, _B), ("win", 5120, _B),
                       ("now", 1024, _B), ("nb", 1024, _B), ("kb", 128, _F), ("kc", 128, _F), ("k4", 64, _I), ("ka", 64, _I),
                       ("kv", 64, _I), ("w", 64, _F), ("o", 64, _F), ("ou", 64, _U), ("d", 64, _F), ("rr", 64, _I),
                       ("a2", 1024, _B), ("nf", 64, _F), ("q", 64, _F), ("df", 64, _F), ("a3", 1024, _B), ("c3", 1024, _B), ("mm", 64, _I)):
        SCRATCH[_n + "_%d" % _k] = ("sbuf", [128, _c], _d)
NDMA = 16
SEMAPHORES = ["sV", "sS", "sP", "sG", "ls", "arr0", "arr1", "arr2"] + ["d%d" % k for k in range(NDMA)]

CY = 0.000833
GA = 1.47
PEC = 0.00053
WAKE = 0.069
BONUS = {"nearer": 4.0, "loop": -3.2, "score": -7.1, "nk-": -5.2, "now||": -1.0, "cnt3": 5.2, "XM'": -0.3, "ac||": 0.1, "now-": 0.9,
         "nk||": 3.4, "ac-": -2.2, "df": -0.6, "c5||": 0.9, "c3": -0.3, "rf": 5.4, "cand||": 0.1, "u": 2.1, "XR'": -1.2, "me": -0.8,
         "cand": 1.0, "c5-": -1.6, "v": -1.8, "dist": -0.1, "kmin": 3.7}
VIAS = (0, 1, 2, 3)
VW = 128
NET = 5.5
XMV = "SSSSSSSSSS"
TAIL = 4 * ROUNDS - 1
FIRST = ((0, 66, "S"), (66, 130, "V"), (130, 194, "S"), (194, 256, "S"))


def _span(r):
    return r[0], r[1], r[2]


def _ap(T, r):
    if len(r) == 4:
        return T[r[0]][:, r[1]:r[2]:r[3]]
    return T[r[0]][:, r[1]:r[2]]


def _count(r):
    return (r[2] - r[1] + (r[3] - 1 if len(r) == 4 else 0)) // (r[3] if len(r) == 4 else 1)


def _psum(name):
    return SCRATCH[name][0] == "psum" if name in SCRATCH else False


def design():
    ops = []

    def op(eng, f, rd, wr, dur, lat=WAKE, name="", **kw):
        o = {"eng": eng, "f": f, "rd": [_span(r) for r in rd], "wr": [_span(r) for r in wr], "dur": dur, "lat": lat, "name": name}
        o.update(kw)
        ops.append(o)

    def tt(out, a, b, alu, name="tt"):
        c = 1 if (_psum(a[0]) or _psum(b[0])) else 2
        op("V", lambda q, T: q.tensor_tensor(_ap(T, out), _ap(T, a), _ap(T, b), alu), [a, b], [out],
           0.02 + CY * max(64, c * _count(out)), name=name)

    def ts(out, a, s1, s2, op0, op1=None, name="ts"):
        aps = [s for s in (s1, s2) if isinstance(s, tuple)]
        two = all(SCRATCH[r[0]][2] in (_B, _U) for r in (out, a))

        def f(q, T):
            x1 = _ap(T, s1) if isinstance(s1, tuple) else s1
            x2 = _ap(T, s2) if isinstance(s2, tuple) else s2
            if op1 is None:
                return q.tensor_scalar(_ap(T, out), _ap(T, a), x1, None, op0)
            return q.tensor_scalar(_ap(T, out), _ap(T, a), x1, x2, op0, op1)
        op("V", f, [a] + aps, [out], 0.02 + CY * max(64, (0.5 if two else 1) * _count(out)), name=name)

    def copy(out, a, name="copy"):
        op("V", lambda q, T: q.tensor_copy(_ap(T, out), _ap(T, a)), [a], [out], 0.02 + CY * max(64, _count(out)), name=name)

    def memset(buf, lo, hi, val, p0=0, p1=128):
        op("V", lambda q, T: q.memset(T[buf][p0:p1, lo:hi], val), [], [(buf, lo, hi)], 0.02 + CY * max(64, 0.5 * (hi - lo)), name="memset")

    def gtt(out, win, off, b, alu, name):
        op("V", lambda q, T: q.tensor_tensor(_ap(T, out), _ap(T, win).indirect(_ap(T, off)), _ap(T, b), alu), [win, off, b], [out],
           0.05 + CY * GA * _count(out), name=name)

    def gather(out, win, off, name, eng="S"):
        def f(q, T, e):
            if e == "V":
                return q.tensor_copy(_ap(T, out), _ap(T, win).indirect(_ap(T, off)))
            return q.activation(_ap(T, out), _ap(T, win).indirect(_ap(T, off)), ActivationFunctionType.Copy)
        op(eng, f, [win, off], [out], 0.06 + CY * GA * _count(out), name=name, flex=True)

    def absS(out, a, name):
        op("S", lambda q, T: q.activation(_ap(T, out), _ap(T, a), ActivationFunctionType.Abs), [a], [out],
           0.1 + CY * _count(out), name=name)

    def sub(out, a, b, name):
        def f(q, T):
            n = out[2] - out[1]
            for s in range(0, n, BANK):
                e = min(n, s + BANK)
                q.matmul(T[out[0]][:, out[1] + s:out[1] + e], T["ident"][:], T[a[0]][:, a[1] + s:a[1] + e], True, False)
                i = q.matmul(T[out[0]][:, out[1] + s:out[1] + e], T["nident"][:], T[b[0]][:, b[1] + s:b[1] + e], False, True)
            return i
        op("P", f, [a, b, ("ident", 0, 128), ("nident", 0, 128)], [out], PEC * 2 * _count(out), name=name)

    def total(out, a, wb, const, name, *more):
        def f(q, T):
            o = _ap(T, out)
            if const is not None:
                q.matmul(o, T["ones"][:], T[const[0]][:, const[1]:const[1] + out[2] - out[1]], True, False)
            todo = [(x, p) for x in (a,) + more for p in range(16)]
            for n, (x, p) in enumerate(todo):
                i = q.matmul(o, T[wb][:, 15 - p:143 - p], T[x[0]][:, x[1] + p:x[2]:16], const is None and n == 0, n == len(todo) - 1)
            return i
        op("P", f, [a, (wb, 0, 144), ("ones", 0, 128)] + list(more) + ([(const[0], const[1], const[1] + 64)] if const else []), [out],
           PEC * 64 * (16 * (1 + len(more)) + (1 if const else 0)), name=name)

    nd = [0]

    def dma(q, fo, fi, rd, wr, name, nbytes=0):
        k = nd[0]
        nd[0] += 1
        op(q, lambda e, T: e.dma_start(fo(T), fi(T)), rd, wr, 0.06, lat=2.0 + nbytes / 200e3, name=name, dma="d%d" % k)

    dma("S", lambda T: T.fl[:, 0:W], lambda T: T.flood[:], [], [("fl", 0, W)], "ld flood", 524288)
    dma("Y", lambda T: T["rn_0"][:, 0:P], lambda T: T.riv[:], [], [("rn_0", 0, P)], "ld riv", 131072)
    dma("Y", lambda T: T["mn_0"][:, 0:P], lambda T: T.bord[:], [], [("mn_0", 0, P)], "ld bord", 131072)
    dma("Y", lambda T: T.thi[:], lambda T: T.th[:], [], [("thi", 0, 1)], "ld th")
    dma("Y", lambda T: T.epi[:], lambda T: T.eps[:], [], [("epi", 0, 1)], "ld eps")
    dma("S", lambda T: T.fl[:, W:W + FW], lambda T: T.flood[:, 0:FW], [], [("fl", W, W + FW)], "ld flood2", 414000)
    iota = lambda out, pat, base, cm, dtype=_I: op(
        "G", lambda q, T: q.iota(_ap(T, out), pat, base, cm, allow_small_or_imprecise_dtypes=True) if dtype == _F else q.iota(_ap(T, out), pat, base, cm),
        [], [out], 0.13 + 2 * CY * _count(out), name="iota")

    def asel(out, a, pat, cmp, base, cm):
        op("G", lambda q, T: q.affine_select(_ap(T, out), _ap(T, a), pat, cmp, 0.0, base, cm), [a], [out], 0.17 + 2 * CY * _count(out), name="asel")

    memset("ones", 0, 128, 1.0)
    iota(("ipt", 0, 64), [[0, 64]], 0, 1)
    iota(("i16", 0, 64), [[16, 64]], 0, 0)
    asel(("ident", 0, 128), ("ones", 0, 128), [[-1, 128]], OP.is_equal, 0, 1)
    asel(("g8", 0, 8), ("ones", 0, 8), [[-16, 8]], OP.is_ge, 0, 1)
    asel(("g8b", 0, 8), ("g8", 0, 8), [[16, 8]], OP.is_ge, 15, -1)
    iota(("iot", 0, 256), [[1, 256]], 0, 0, _F)
    iota(("dgi", 0, 512), [[0, 32], [1, 16]], 0, -1)
    iota(("dgj", 0, 512), [[0, 32], [1, 16]], 0, 0)
    ts(("nident", 0, 128), ("ident", 0, 128), -1.0, None, OP.mult)
    memset("b1", 0, 144, 0.0)
    copy(("b1", 15, 143, 16), ("g8b", 0, 8))
    for w in (8192, 16384, 4096):
        ts(("b%d" % w, 0, 144), ("b1", 0, 144), float(w), None, OP.mult)
    memset("ck", 0, 320, -262144.0, 0, 64)
    for m in range(4):
        memset("ck", 64 * m, 64 * m + 64, 32.0 * m, 64, 128)
    memset("ck", 256, 320, 128.0, 64, 128)
    cons = [(77 * t - 592) % W for t in range(ROUNDS)]
    memset("cy", 0, 192, -2176.0, 0, 64)
    for t in range(ROUNDS):
        x = cons[t] / 32.0
        hi = int(x * 4) / 4.0
        memset("cy", 64 * t, 64 * t + 64, hi, 64, 96)
        memset("cy", 64 * t, 64 * t + 64, x - hi, 96, 128)
    memset("cz", 0, 64, -544.0, 0, 64)
    memset("cz", 64, 128, -1568.0, 0, 64)
    memset("cz", 0, 128, 0.0, 64, 128)
    ts(("ip2", 0, 64), ("ipt", 0, 64), 15, None, OP.bitwise_and)
    tt(("cpos", 0, 64), ("ip2", 0, 64), ("i16", 0, 64), OP.add)
    POS, IOT = ("pv", 0, 64), ("pv", 64, 128)
    copy(POS, ("cpos", 0, 64))
    copy(IOT, ("iot", 0, 64))
    ts(("cpos", 0, 64), ("cpos", 0, 64), 4096.0, None, OP.add)
    ts(("dgi", 0, 512), ("dgi", 0, 512), 15, None, OP.bitwise_and)
    ts(("diag", 0, 512), ("dgi", 0, 512), 0.0, None, OP.is_equal)
    ts(("seg", 0, 512), ("dgj", 0, 512), 0.0, None, OP.is_gt)
    copy(("tha", 0, 1), ("thi", 0, 1))
    copy(("epf", 0, 1), ("epi", 0, 1))
    ts(("epf", 1, 2), ("epi", 0, 1), -1.0, None, OP.mult)
    for k in range(2):
        memset("rf_%d" % k, 257, 264, 592.0)
        memset("mf_%d" % k, 256, 264, 592.0)
        memset("rp_%d" % k, 256, 296, -4096)
        memset("xr_%d" % k, 4096, 4112, 0.0)

    FL = ("fl", 0, W)
    FL2 = ("fl", 0, W + FW)
    for lo, hi, e in FIRST:
        copy(("ru0", lo, hi), ("rn_0", lo, hi), "R u16")
        gather(("xr_0", 16 * lo, 16 * hi), FL, ("ru0", lo, hi), "XR0", e)
    ts(("rf_0", 1, 257), ("rn_0", 0, 256), 592.0, None, OP.add)
    copy(("rf_0", 0, 1), ("rf_0", 1, 2))
    ts(("mf_0", 0, 256), ("mn_0", 0, 256), 592.0, None, OP.add)
    for lo, hi in ((0, 64), (64, 128), (128, 192), (192, 256)):
        copy(("mu_0", lo, hi), ("mn_0", lo, hi), "M u16")
        gather(("xm", 16 * lo, 16 * hi), FL, ("mu_0", lo, hi), "XM0")

    nkc = [0]

    def nkcol():
        c = nkc[0]
        nkc[0] += 1
        return ("nk", c, c + 1)
    neck = {}

    def halves(lo, hi, yes):
        if not yes or hi - lo <= 32:
            return [(lo, hi)]
        m = (lo + hi) // 2
        return [(lo, m), (m, hi)]

    def step1(t, k):
        s = (4 * t + k) % 2
        z = t % 2
        b = lambda n: n + "_%d" % s
        c0 = CK * k
        rn, rf, mn, mf = "rn_%d" % z, "rf_%d" % z, "mn_%d" % z, "mf_%d" % z
        xr = "xr_%d" % z
        R16, K12, M5, UU = ("pv", 128, 192), ("pv", 192, 320), ("pv", 320, 384), ("pv", 384, 448)
        T5, ZZ, K2 = ("pv", 192, 256), ("pv", 256, 320), ("pv", 256, 320)
        xn = (xr, 16 * (c0 + 1), 16 * (c0 + 65))
        sc = "sc%d" % s
        ts(R16, (rn, c0, c0 + 64), 16.0, None, OP.add, name="R16")
        for m, (bf, o) in enumerate(((rf, c0), (rf, c0 + 2), (mf, c0), (mf, c0 + 1))):
            tt((b("pr"), 64 * m, 64 * m + 64), R16, (bf, o, o + 64), OP.mult, name="prod")
        for h in range(0, 256, VW):
            ts((b("v"), h, h + VW), (b("pr"), h, h + VW), 4, W - 1, OP.arith_shift_right, OP.bitwise_and, name="v")
            ts((b("u"), h, h + VW), (b("v"), h, h + VW), float(cons[t]), None, OP.add, name="u")
        sub(("sub0", 0, CE), (xr, 16 * c0, 16 * (c0 + 64)), xn, "now-")
        absS((b("now"), 0, CE), ("sub0", 0, CE), "now||")
        sub(("sub0", 0, CE), ("xm", 16 * c0, 16 * (c0 + 64)), xn, "c5-")
        absS((b("win"), 4 * CE, 5 * CE), ("sub0", 0, CE), "c5||")
        for m in range(4):
            gtt((b("xd"), CE * m, CE * m + CE), FL2, (b("u"), 64 * m, 64 * m + 64), xn, OP.subtract, "cand")
            absS((b("win"), CE * m, CE * m + CE), (b("xd"), CE * m, CE * m + CE), "cand||")
        for m in (4, 0, 1, 2, 3):
            total((sc, 64 * m, 64 * m + 64), (b("win"), CE * m, CE * m + CE), "b8192", ("ck", 64 * m), "score")
        tt(K12, (sc, 0, 128), (b("v"), 0, 128), OP.add, "key")
        tt((b("kb"), 0, 128), (sc, 128, 256), (b("v"), 128, 256), OP.add, "key")
        tt((b("kc"), 0, 64), ("pv", 192, 256), (b("kb"), 0, 64), OP.min, "kmin")
        tt(K2, K2, (b("kb"), 64, 128), OP.min, "kmin")
        tt((b("k4"), 0, 64), K2, (b("kc"), 0, 64), OP.min, "kmin")
        tt(M5, (sc, 256, 320), (b("k4"), 0, 64), OP.is_le, "m5")
        ts((b("ka"), 0, 64), (b("k4"), 0, 64), 6144, 1, OP.bitwise_and, OP.arith_shift_right, name="ka")
        tt(UU, M5, ("cpos", 0, 64), OP.mult, "uu")
        tt((b("w"), 0, 64), POS, (b("ka"), 0, 64), OP.add, "w")
        tt((b("o"), 0, 64), UU, (b("w"), 0, 64), OP.max, "o")
        copy((b("ou"), 0, 64), (b("o"), 0, 64), "ou")
        gtt((b("nb"), 0, CE), (b("win"), 0, 5 * CE), (b("ou"), 0, 64), (b("now"), 0, CE), OP.is_lt, "nearer")
        ts((b("kv"), 0, 64), (b("k4"), 0, 64), W - 1, None, OP.bitwise_and, name="kv")
        ts((b("me"), 0, 64), (mn, c0, c0 + 64), 4096.0 - cons[t], None, OP.add, name="me")
        tt(T5, M5, (b("me"), 0, 64), OP.mult, "t5")
        tt((b("d"), 0, 64), T5, (b("kv"), 0, 64), OP.max, "d")
        total((sc, 320, 384), (b("nb"), 0, CE), "b16384", ("cy", 64 * t), "cnt1")
        tt(ZZ, (sc, 320, 384), (b("d"), 0, 64), OP.add, "z")
        tt((b("rr"), 0, 64), ZZ, (rn, c0, c0 + 64), OP.max, "rr")
        rp, rpu = "rp_%d" % z, "rpu_%d" % z
        e = 63 if k == 3 else 64
        ts((rp, c0, c0 + e), (b("rr"), 0, e), W - 1, None, OP.bitwise_and, name="R'")
        if k == 3:
            copy((rp, 255, 256), (rn, 255, 256), "R'255")
        copy((rpu, c0, c0 + 64), (rp, c0, c0 + 64), "R'u")
        for a, c in halves(c0, c0 + 64, 4 * t + k >= TAIL):
            gather(("xp", 16 * a, 16 * c), FL, (rpu, a, c), "XR'", "VS" if 4 * t + k >= TAIL else "S")

    def necks(t, k):
        s = (4 * t + k) % 2
        b = lambda n: n + "_%d" % s
        lo, hi = max(0, 64 * k - 32), 64 * k + 32
        n = hi - lo
        for a, c in halves(lo, hi, 4 * t + k >= TAIL):
            h0, h1 = 16 * (a - lo), 16 * (c - lo)
            sub(("sub1", h0, h1), ("xp", 16 * a, 16 * c), ("xp", 16 * (a + 32), 16 * (c + 32)), "nk-")
            absS((b("a2"), h0, h1), ("sub1", h0, h1), "nk||")
        total(("cnt", 0, n), (b("a2"), 0, 16 * n), "b1", None, "dist")
        ts((b("nf"), 0, n), ("cnt", 0, n), ("tha", t, t + 1), 256.0, OP.is_ge, OP.mult, name="nf")
        tt((b("q"), 0, n), ("pv", 64, 64 + n), (b("nf"), 0, n), OP.add, "q")
        m = nkcol()
        qq = (b("q"), 0, n)
        op("V", lambda e, T: e.tensor_reduce(_ap(T, m), _ap(T, qq), AxisListType.X, OP.min), [qq], [m], 0.02 + CY * 64, name="red")
        m2 = nkcol()
        ts(m2, m, float(lo), neck[t, k - 1] if k else 256.0, OP.add, OP.min, name="nk")
        neck[t, k] = m2

    def loops(t):
        z = t % 2
        nk = neck[t, 3]
        lout = "lout%d" % t
        ts(("lu", 0, 32), ("iot", 0, 32), nk, 1.0, OP.add, OP.add, name="lu")
        gtt(("lg", 0, 512), ("rp_%d" % z, 0, 296), ("lu", 0, 32), ("diag", 0, 512), OP.mult, "loop")
        op("V", lambda e, T: e.tensor_tensor_scan(T.ls[:], T.seg[:], T.lg[:], 0.0, OP.mult, OP.add), [("seg", 0, 512), ("lg", 0, 512)], [("ls", 0, 512)],
           0.02 + CY * 512, name="scan")
        copy((lout, 0, 32), ("ls", 15, 512, 16), "lout")
        op("G", None, [(lout, 0, 32)], [], 1.0, name="send", send=t)
        op("N", None, [(lout, 0, 32)], [("land%d" % t, 0, 32)], 0.0, lat=NET, name="recv", recv=t)
        ts(("tha", 4 + t, 5 + t), nk, 256.0, 16.0, OP.is_lt, OP.mult, name="A")
        tt(("tha", t + 1, t + 2), ("tha", t, t + 1), ("tha", 4 + t, 5 + t), OP.add, "A")

    def landed(t):
        rp, lout = ("rp_%d" % (t % 2), 224, 256), ("lout%d" % t, 0, 32)
        ts(("lm", 0, 32), ("iot", 224, 256), neck[t, 3], None, OP.is_gt, name="l0")
        tt(("lo", 0, 32), lout, rp, OP.subtract, "l0")
        tt(("lo", 0, 32), ("lo", 0, 32), ("lm", 0, 32), OP.mult, "l0")
        tt(("lo", 0, 32), ("lo", 0, 32), rp, OP.add, "l0")
        ts(("lm", 0, 32), ("lm", 0, 32), 1.0, 8192.0, OP.subtract, OP.mult, name="l0")
        tt(("l1", 0, 32), ("land%d" % t, 0, 32), ("lm", 0, 32), OP.add, "l1")
        ts(("l2", 0, 32), ("l1", 0, 32), 0.0, -8192.0, OP.is_ge, OP.mult, name="l1")
        tt(("l2", 0, 32), ("l2", 0, 32), ("lo", 0, 32), OP.add, "l2")

    def moved(t, k):
        s = (4 * t + k) % 2
        b = lambda n: n + "_%d" % s
        z, y = t % 2, (t + 1) % 2
        last = t == ROUNDS - 1
        cn, c0 = ("sc0", 0) if last and k < 4 else ("cnt", 64)
        lo, hi = (max(0, 64 * k - 32), 64 * k + 32) if k < 4 else (224, 256)
        n = hi - lo
        rp = "rp_%d" % z
        rn = ("yrf", lo, hi) if last else ("rn_%d" % y, lo, hi)
        MK = ("pv", 448, 448 + n)
        if k < 4:
            tt((b("df"), 0, n), (rp, lo + 32, hi + 32), (rp, lo, hi), OP.subtract, "df")
            ts(MK, ("iot", lo, hi), neck[t, k], None, OP.is_gt, name="mk")
            tt(MK, MK, (b("df"), 0, n), OP.mult, "dm")
            tt(rn, MK, (rp, lo, hi), OP.add, "R''")
        else:
            tt(rn, ("l2", 0, 32), ("l1", 0, 32), OP.max, "R''")
        u = ("r2u_%d" % z, lo, hi)
        copy(u, rn, "R''u")
        if last and k in VIAS:
            x = ("xr_%d" % y, 16 * lo, 16 * hi)
            gather(x, FL, u, "XR''")
            sub(("sub0", 0, 16 * n), x, ("xm", 16 * lo, 16 * hi), "ac-")
            absS((b("a3"), 0, 16 * n), ("sub0", 0, 16 * n), "ac||")
            ts((b("c3"), 0, 16 * n), (b("a3"), 0, 16 * n), ("epf", 0, 1), None, OP.is_le, name="c3")
            total((cn, c0, c0 + n), (b("c3"), 0, 16 * n), "b4096", ("cz", 0), "cnt3")
        elif last:
            x3, c3, c4 = (b("a3"), 0, 16 * n), (b("c3"), 0, 16 * n), (b("nb"), 0, 16 * n)
            gtt(x3, FL, u, ("xm", 16 * lo, 16 * hi), OP.subtract, "cand")
            ts(c3, x3, ("epf", 0, 1), None, OP.is_le, name="c3")
            ts(c4, x3, ("epf", 1, 2), None, OP.is_ge, name="c3")
            total((cn, c0, c0 + n), c3, "b4096", ("cz", 64), "cnt3", c4)
        else:
            gather(("xr_%d" % y, 16 * lo, 16 * hi), FL, u, "XR''")
        if not last:
            rf = "rf_%d" % y
            ts((rf, lo + 1, hi + 1), rn, 592.0, None, OP.add, name="rf")
            if k == 0:
                copy((rf, 0, 1), (rf, 1, 2), "rf0")
            sub(("sub1", 0, 16 * n), ("xr_%d" % y, 16 * lo, 16 * hi), ("xm", 16 * lo, 16 * hi), "ac-")
            absS((b("a3"), 0, 16 * n), ("sub1", 0, 16 * n), "ac||")
            ts((b("c3"), 0, 16 * n), (b("a3"), 0, 16 * n), ("epf", 0, 1), None, OP.is_le, name="c3")
            total((cn, c0, c0 + n), (b("c3"), 0, 16 * n), "b4096", ("cz", 0), "cnt3")
        Z3 = ("pv", 448, 448 + n)
        tt(Z3, (cn, c0, c0 + n), rn, OP.add, "z3")
        tt((b("mm"), 0, n), Z3, ("mn_%d" % z, lo, hi), OP.max, "mm")
        mn = ("mn_%d" % y, lo, hi)
        ts(mn, (b("mm"), 0, n), W - 1, None, OP.bitwise_and, name="M'")
        if last:
            copy(("ymf", lo, hi), mn, "M f")
            return
        ts(("mf_%d" % y, lo, hi), mn, 592.0, None, OP.add, name="mf")
        mu = ("mu_%d" % y, lo, hi)
        copy(mu, mn, "M'u")
        gather(("xm", 16 * lo, 16 * hi), FL, mu, "XM'", XMV[5 * t + k])

    for slot in range(4 * ROUNDS + 3):
        if slot < 4 * ROUNDS:
            step1(slot // 4, slot % 4)
        e = slot - 1
        if 0 <= e < 4 * ROUNDS:
            t, k = divmod(e, 4)
            necks(t, k)
            if k == 3:
                loops(t)
            if t < ROUNDS - 1:
                moved(t, k)
            elif k == 3:
                for j in range(4):
                    moved(t, j)
        f = slot - 2
        if f >= 0 and f % 4 == 3 and f < 4 * ROUNDS:
            landed(f // 4)
            moved(f // 4, 4)
    tt(("aout", 0, 1), ("tha", ROUNDS, ROUNDS + 1), ("tha", 0, 1), OP.subtract)
    ts(("aout", 1, 2), ("aout", 0, 1), 0.0625, None, OP.mult)
    dma("Y", lambda T: T.ya[:], lambda T: T.aout[:, 1:2], [("aout", 1, 2)], [], "st ya")
    dma("Y", lambda T: T.yr[:, 0:224], lambda T: T.yrf[:, 0:224], [("yrf", 0, 224)], [], "st yr")
    dma("Y", lambda T: T.ym[:, 0:224], lambda T: T.ymf[:, 0:224], [("ymf", 0, 224)], [], "st ym")
    dma("Y", lambda T: T.yr[:, 224:256], lambda T: T.yrf[:, 224:256], [("yrf", 224, 256)], [], "st yr")
    dma("Y", lambda T: T.ym[:, 224:256], lambda T: T.ymf[:, 224:256], [("ymf", 224, 256)], [], "st ym")
    return ops


def depend(ops):
    acc = {}
    for i, o in enumerate(ops):
        dep = set()
        touches = [(r, False) for r in o["rd"]] + [(r, True) for r in o["wr"]]
        for (buf, lo, hi), wr in touches:
            lst = acc.setdefault(buf, [])
            ps = _psum(buf)
            for (j, l2, h2, w2) in lst:
                if j == i:
                    continue
                hit = lo < h2 and l2 < hi and (wr or w2)
                if ps and not hit:
                    hit = ops[j]["eng"] != o["eng"] and lo // BANK <= (h2 - 1) // BANK and l2 // BANK <= (hi - 1) // BANK
                if hit:
                    dep.add(j)
        for (buf, lo, hi), wr in touches:
            lst = acc[buf]
            if wr and not _psum(buf):
                lst[:] = [a for a in lst if not (lo <= a[1] and a[2] <= hi)]
            lst.append((i, lo, hi, wr))
        o["dep"] = dep


def arrange(ops):
    n = len(ops)
    succ = [[] for _ in range(n)]
    for i, o in enumerate(ops):
        for j in o["dep"]:
            succ[j].append(i)
    rank = [0.0] * n
    for i in range(n - 1, -1, -1):
        o = ops[i]
        rank[i] = o["dur"] + o["lat"] + max([rank[j] for j in succ[i]], default=0.0)
    for i, o in enumerate(ops):
        rank[i] += BONUS.get(o["name"], 0.0)
    left = [len(o["dep"]) for o in ops]
    at = [0.0] * n
    free = {"V": 0.0, "S": 0.0, "P": 0.0, "G": 0.0, "Y": 0.0, "N": 0.0}
    ready = {e: [] for e in free}

    def push(i):
        for e in ops[i]["eng"]:
            ready[e].append(i)
    for i in range(n):
        if not left[i]:
            push(i)
    order = {e: [] for e in free}
    done = 0
    end = 0.0
    while done < n:
        best = None
        for e in free:
            if ready[e]:
                t = max(free[e], min(at[i] for i in ready[e]))
                if best is None or t < best[0]:
                    best = (t, e)
        t, e = best
        i = max((j for j in ready[e] if at[j] <= t), key=lambda j: (rank[j], -j))
        o = ops[i]
        for x in o["eng"]:
            ready[x].remove(i)
        o["on"] = e
        o["t0"] = t
        order[e].append(i)
        free[e] = t + o["dur"] if e != "N" else 0.0
        f = t + o["dur"] + o["lat"]
        end = max(end, f)
        done += 1
        for j in succ[i]:
            at[j] = max(at[j], f)
            left[j] -= 1
            if not left[j]:
                push(j)
    return order, end


_made = {}


def made():
    if not _made:
        ops = design()
        depend(ops)
        order, end = arrange(ops)
        _made["ops"], _made["order"], _made["end"] = ops, order, end
        num = {}
        for e in "VSPG":
            c = 0
            for i in order[e]:
                if "dma" in ops[i] or "send" in ops[i]:
                    continue
                c += 1
                num[i] = c
        _made["num"] = num
        seq = sorted(range(len(ops)), key=lambda i: (ops[i]["t0"], i))
        pos = {i: n for e in order for n, i in enumerate(order[e])}
        state = {e: {} for e in order}
        after = {}
        waits = {}
        todo = {e: 0 for e in order}
        ndone = 0
        while ndone < len(seq):
            for e in order:
                while todo[e] < len(order[e]) and all(j in after for j in ops[order[e][todo[e]]]["dep"]):
                    i = order[e][todo[e]]
                    o = ops[i]
                    st = state[e] if e != "N" else {}
                    need = {}
                    for j in o["dep"]:
                        key, val = _key(j, ops, num)
                        if key is not None and st.get(key, 0) < val and need.get(key, (0, 0))[0] < val:
                            need[key] = (val, j)
                    out = []
                    for key, (val, j) in sorted(need.items(), key=lambda kv: -pos[kv[1][1]]):
                        if st.get(key, 0) >= val:
                            continue
                        out.append((key, val))
                        for a, c in after[j].items():
                            st[a] = max(st.get(a, 0), c)
                        st[key] = max(st.get(key, 0), val)
                    waits[i] = out
                    me = dict(st)
                    key, val = _key(i, ops, num)
                    if key is not None:
                        me[key] = val
                    after[i] = me
                    todo[e] += 1
                    ndone += 1
        _made["waits"] = waits
    return _made


def _key(i, ops, num):
    o = ops[i]
    if "dma" in o:
        return o["dma"], 16
    if "send" in o:
        return None, 0
    if "recv" in o:
        return "arr%d" % o["recv"], 8
    return "s" + o["on"], num[i]


def rank_program(g, core, T, topo):
    rank = T.rank_of(core)
    if rank is None:
        return
    m = made()
    ops, order, waits = m["ops"], m["order"], m["waits"]
    queues = {"V": g.vector, "S": g.scalar, "P": g.tensor, "G": g, "Y": g.sync}
    sent = 0
    for e in ("G", "Y", "S", "V", "P"):
        q = queues[e]
        for i in order[e]:
            o = ops[i]
            for key, val in waits[i]:
                q.wait_ge(T.sem[key], val)
            if "send" in o:
                t = o["send"]
                dst = T.cores[(rank + 1 + t % (N - 1)) % N]
                rid, pid, _ = topo.addr(dst)
                eng = topo.engines(core, dst)[:8]
                g.remote_dma(out_ap=T["land%d" % t][:], in_ap=T["lout%d" % t][:], remote_sem=T.sem["arr%d" % t], local_sem=T.sem.ls,
                             pid=pid, routing_id=rid, dma_engine_mask=sum(1 << x for x in eng))
                sent += len(eng)
            elif "dma" in o:
                o["f"](q, T).then_inc(T.sem[o["dma"]], 16)
            elif "flex" in o:
                o["f"](q, T, e).then_inc(T.sem["s" + e], 1)
            else:
                o["f"](q, T).then_inc(T.sem["s" + e], 1)
    g.wait_ge(T.sem.ls, sent)
    for i, o in enumerate(ops):
        if "dma" in o and o["name"].startswith("st"):
            g.sync.wait_ge(T.sem[o["dma"]], 16)
    for e in "VSPG":
        g.sync.wait_ge(T.sem["s" + e], max(c for i, c in m["num"].items() if ops[i]["on"] == e))
